import numpy as np
import ml_dtypes


def mxq(x, axis, fmt="e4m3"):
    dtype, down = {"e4m3": (ml_dtypes.float8_e4m3fn, 7), "e5m2": (ml_dtypes.float8_e5m2, 14)}[fmt]
    v = np.moveaxis(np.asarray(x, np.float32).astype(ml_dtypes.bfloat16).astype(np.float64), axis, -1)
    blocks = v.reshape(v.shape[:-1] + (-1, 32))
    amax = np.abs(blocks).max(-1, keepdims=True)
    byte = np.maximum(np.where(amax > 0, np.frexp(amax)[1] - 1 + 127, 0) - down, 1)
    scale = np.exp2(byte - 127.0)
    codes = (blocks / scale).astype(np.float32).astype(dtype).astype(np.float64)
    return np.moveaxis((codes * scale).reshape(v.shape), -1, axis)


WIDE = False


def mx_kscale(k):
    if not WIDE:
        return np.ones(k)
    levels = np.array([10, -10, 5, -5, 0])
    if k % 512:
        return np.exp2(np.random.permutation(np.resize(levels, k // 32))).repeat(32)
    a = np.empty((k // 512, 16))
    for p in range(k // 512):
        a[p, :8] = np.random.permutation(np.resize(levels, 8))
        for g in range(8):
            far = levels[np.abs(levels - a[p, g]) >= 10]
            a[p, g + 8] = far[np.random.randint(len(far))]
    return np.exp2(a.ravel()).repeat(32)


def f64(x):
    return np.asarray(x).astype(np.float64)


def striped(idx):
    return np.tile(np.asarray(idx).reshape(-1, 16).T, (8, 1)).astype(np.uint16)


def unstriped(offs):
    return offs[:16].T.reshape(-1).astype(np.int64)


E2M1 = np.array([0.0, 0.5, 1.0, 1.5, 2.0, 3.0, 4.0, 6.0, -0.0, -0.5, -1.0, -1.5, -2.0, -3.0, -4.0, -6.0])


def pack_weight(w, fmt):
    k, n = w.shape
    w = f64(np.asarray(w, np.float32).astype(ml_dtypes.bfloat16)).reshape(k // 32, 32, n)
    amax = np.abs(w).max(1)
    if fmt == "e4m3":
        byte = np.frexp(amax)[1] - 1 + 127 - 7
    else:
        mant, ex = np.frexp(amax / 6.0)
        byte = np.where(mant > 0.5, ex, ex - 1) + 127
    byte = np.clip(np.where(amax > 0, byte, 1), 1, 254)
    scaled = (w * np.exp2(127.0 - byte)[:, None, :]).reshape(k, n).astype(np.float32)
    by_word = np.ascontiguousarray(scaled.reshape(k // 512, 128, 4, n).transpose(0, 1, 3, 2))
    if fmt == "e4m3":
        words = by_word.astype(ml_dtypes.float8_e4m3fn).view(np.uint8)
    else:
        c = by_word.astype(ml_dtypes.float4_e2m1fn).view(np.uint8) & 0xF
        words = (c[..., 0::2] | (c[..., 1::2] << 4)).reshape(k // 512, 128, 2 * n)
    return np.ascontiguousarray(words), np.ascontiguousarray(byte.astype(np.uint8).reshape(k // 512, 16, n))


def unpack_weight(words, scales, fmt):
    g, _, n = scales.shape
    words = np.ascontiguousarray(words).reshape(g, 128, n, -1)
    if fmt == "e4m3":
        vals = words.view(ml_dtypes.float8_e4m3fn).astype(np.float64)
    else:
        nib = np.empty((g, 128, n, 4), np.uint8)
        nib[..., 0::2] = words & 0xF
        nib[..., 1::2] = words >> 4
        vals = E2M1[nib]
    vals = vals * np.repeat(np.exp2(scales.astype(np.float64) - 127.0), 8, axis=1)[..., None]
    return vals.transpose(0, 1, 3, 2).reshape(g * 512, n)


B, N, T, D, DV, NQ = 1, 1024, 4096, 512, 256, 128
PAGE = 512
CAP = 2.0


def setup_inputs():
    n = np.random.standard_normal
    pages = np.random.permutation(T // PAGE)[:B * N // PAGE]
    idx = (pages[:, None] * PAGE + np.arange(PAGE)[None, :]).reshape(-1)
    s = mx_kscale(D)[:, None]
    u = np.ones(T)
    u[idx] = mx_kscale(B * N)
    r = np.random.uniform(0.5, 2.0, T)
    qp = [pack_weight(x, "e4m3") for x in n((B, D, NQ)) * s * (1.00 / np.sqrt(D))]
    k = n((D, T)) / s
    v = n((DV, T)) / (u * r)
    kp = pack_weight(k, "e4m3")
    vp = pack_weight(v.T, "e4m3")
    return {
        "q_words": np.stack([x[0] for x in qp]),
        "q_scales": np.stack([x[1] for x in qp]),
        "k_words": kp[0],
        "k_scales": kp[1],
        "v_words": vp[0],
        "v_scales": vp[1],
        "vs": np.tile(u * r, (128, 1)).astype(np.float32),
        "offs": striped(idx),
        "voffs": striped((pages[:, None] * DV + np.arange(DV)[None, :]).reshape(-1)),
    }


def reference(q_words, q_scales, k_words, k_scales, v_words, v_scales, vs, offs, voffs):
    idx = unstriped(offs)
    k = unpack_weight(k_words, k_scales, "e4m3")
    v = unpack_weight(v_words, v_scales, "e4m3")
    v = v.reshape(T // 512, 512, DV)[unstriped(voffs)[::DV] // DV].reshape(B, N, DV)
    pick = lambda x: x[:, idx].reshape(x.shape[0], B, N).transpose(1, 0, 2)
    q = np.stack([unpack_weight(q_words[b], q_scales[b], "e4m3") for b in range(B)])
    score = q.transpose(0, 2, 1) @ pick(k)
    score = CAP * np.tanh(score / CAP)
    p = 1.0 / (1.0 + np.exp(-score))
    w = p * pick(f64(vs))[:, :1, :]
    y = mxq(w, 2, "e4m3") @ v
    y = y / 16.0
    return y

@@ -1,0 +1,165 @@
+from contextlib import ExitStack
+
+import concourse.mybir as mybir
+from concourse.masks import make_identity
+
+F32 = mybir.dt.float32
+BF16 = mybir.dt.bfloat16
+I32 = mybir.dt.int32
+U32 = mybir.dt.uint32
+U16 = mybir.dt.uint16
+U8 = mybir.dt.uint8
+FP8X4 = mybir.dt.float8_e4m3fn_x4
+ACT = mybir.ActivationFunctionType
+ALU = mybir.AluOpType
+
+P = 128
+PACK = 4
+PAGE = 512
+PAGES = 2
+SLOTS = PAGE * PAGES
+POOL = 4096
+POOL_PAGES = POOL // PAGE
+D = 512
+DV = 256
+NQ = 128
+VS_ROW = P - 1
+V_PLANE = 4
+FLOPS = 2 * NQ * SLOTS * (D + DV)
+BYTES = (POOL * (D + DV) + NQ * D) * 33 // 32 + POOL * 4 + P * (SLOTS + PAGES * DV) // 8 + NQ * DV * 4
+
+
+def tile_attend_pkv8q_sigm_cap_kernel(
+    tc, q_words, q_scales, k_words, k_scales, v_words, v_scales, vs, offs, voffs, out
+):
+    nc = tc.nc
+    with ExitStack() as ctx:
+        sb = ctx.enter_context(tc.tile_pool(name="sb", bufs=1))
+        ps = ctx.enter_context(tc.psum_pool(name="ps", bufs=1))
+
+        offs_t = sb.tile([P, SLOTS // 16], U16, name="offs_t")
+        voffs_t = sb.tile([P, PAGES * DV // 16], U16, name="voffs_t")
+        kw = sb.tile([P, POOL], I32, name="kw")
+        ks = sb.tile([P, POOL], U8, name="ks")
+        vw = sb.tile([P, POOL_PAGES * DV], I32, name="vw")
+        vsc = sb.tile([P, POOL_PAGES * DV], U8, name="vsc")
+        vst = sb.tile([P, POOL], F32, name="vst")
+        qw = sb.tile([P, NQ], I32, name="qw", align_bytes=64)
+        qs = sb.tile([P, NQ], U8, name="qs", align_bytes=64)
+        ident = sb.tile([P, P], F32, name="ident")
+        warm = sb.tile([P, 1], F32, name="warm")
+
+        nc.vector.memset(ks[:].bitcast(I32), 0)
+        nc.vector.memset(qs[:].bitcast(I32), 0)
+        nc.vector.memset(vsc[:].bitcast(I32), 0)
+        nc.vector.memset(vst[0:VS_ROW, :], 0.0)
+        nc.sync.dma_start(offs_t[:], offs)
+        nc.sync.dma_start(vst[VS_ROW : VS_ROW + 1, :], vs[0:1, :])
+        nc.sync.dma_start(qw[:], q_words[0, 0].rearrange("p n t -> p (n t)").bitcast(I32))
+        for r in range(4):
+            nc.sync.dma_start(ks[r:P:32, :].bitcast(I32), k_scales[0, r:16:4, :].bitcast(I32))
+        nc.scalar.dma_start(kw[:], k_words[0].rearrange("p n t -> p (n t)").bitcast(I32))
+        nc.sync.dma_start(voffs_t[:], voffs)
+        for r in range(4):
+            nc.sync.dma_start(qs[r:P:32, :].bitcast(I32), q_scales[0, 0, r:16:4, :].bitcast(I32))
+        make_identity(nc, ident[:])
+        nc.scalar.activation(warm[:], ident[:, 0:1], ACT.Tanh)
+        nc.scalar.dma_start(
+            vw[:].rearrange("p (u e) -> p u e", u=POOL_PAGES),
+            v_words.rearrange("u p e t -> p u (e t)").bitcast(I32),
+        )
+        for r in range(4):
+            nc.gpsimd.dma_start(
+                vsc[V_PLANE + r : P : 32, :].bitcast(I32).rearrange("p (u c) -> p u c", u=POOL_PAGES),
+                v_scales[:, r:16:4, :].bitcast(I32).rearrange("u g c -> g u c"),
+            )
+
+        vsg = sb.tile([P, SLOTS], F32, name="vsg")
+        nc.vector.tensor_copy(vsg[:], vst[:].indirect(offs_t[:]))
+        vs_half = sb.tile([P, PAGES, PACK], F32, name="vs_half")
+        for e in range(PAGES):
+            turned = ps.tile([P, PACK, P], F32, name=f"turned{e}")
+            for t in range(PACK):
+                nc.tensor.transpose(turned[:, t, :], vsg[:, e * PAGE + t : (e + 1) * PAGE : PACK], ident[:])
+            nc.scalar.activation(vs_half[:, e, :], turned[:, :, VS_ROW], ACT.Copy, scale=0.5)
+
+        ksg = sb.tile([P, SLOTS], U8, name="ksg")
+        nc.vector.tensor_copy(ksg[:], ks[:].indirect(offs_t[:]))
+        ksp = sb.tile([P, SLOTS], U8, name="ksp", align_bytes=64)
+        nc.vector.tensor_copy(
+            ksp[:].rearrange("k (e t p) -> k e t p", e=PAGES, t=PACK),
+            ksg[:].rearrange("k (e p t) -> k e t p", e=PAGES, t=PACK),
+        )
+
+        cols = PAGE // 16
+        kg = []
+        for e in range(PAGES):
+            g = sb.tile([P, PAGE], U32, name=f"kg{e}", align_bytes=64)
+            nc.vector.tensor_copy(
+                g[:].rearrange("k (t p) -> k p t", t=PACK),
+                kw[:].bitcast(U32).indirect(offs_t[:, e * cols : (e + 1) * cols]),
+            )
+            kg.append(g)
+
+        vscg = sb.tile([P, PAGES * DV], U8, name="vscg", align_bytes=64)
+        nc.vector.tensor_copy(vscg[:], vsc[:].indirect(voffs_t[:]))
+
+        p2 = []
+        for e in range(PAGES):
+            score = ps.tile([P, PACK, NQ], F32, name=f"score{e}")
+            for t in range(PACK):
+                nc.tensor.matmul_mx(
+                    out=score[:, t, :],
+                    lhsT=kg[e][:, t * P : (t + 1) * P].bitcast(FP8X4),
+                    lhsT_scale=ksp[:, e * PAGE + t * P : e * PAGE + (t + 1) * P],
+                    rhs=qw[:].bitcast(FP8X4),
+                    rhs_scale=qs[:],
+                    start=True,
+                    stop=True,
+                )
+            half_cap = sb.tile([P, NQ, PACK], F32, name=f"half_cap{e}")
+            nc.scalar.activation(half_cap[:], score[:].rearrange("p t q -> p q t"), ACT.Tanh, scale=0.5)
+            th = sb.tile([P, NQ, PACK], F32, name=f"th{e}")
+            pieces = 2
+            step = NQ // pieces
+            for h in range(pieces):
+                nc.scalar.activation(th[:, h * step : (h + 1) * step, :], half_cap[:, h * step : (h + 1) * step, :], ACT.Tanh)
+            p2.append(th)
+
+        vg = sb.tile([P, PAGES * DV], U32, name="vg", align_bytes=64)
+        acc = [ps.tile([P, DV // 2], F32, name=f"acc{c}") for c in range(2)]
+        for e in range(PAGES):
+            w = sb.tile([P, NQ, PACK], BF16, name=f"w{e}", align_bytes=64)
+            for h in range(2):
+                qh = slice(h * (NQ // 2), (h + 1) * (NQ // 2))
+                nc.vector.scalar_tensor_tensor(
+                    out=w[:, qh, :],
+                    in0=p2[e][:, qh, :],
+                    scalar=1.0,
+                    in1=vs_half[:, e, :].unsqueeze(1).to_broadcast([P, NQ // 2, PACK]),
+                    op0=ALU.add,
+                    op1=ALU.mult,
+                )
+            if e == 0:
+                nc.vector.tensor_copy(vg[:], vw[:].bitcast(U32).indirect(voffs_t[:]))
+            wq = sb.tile([P, NQ], U32, name=f"wq{e}", align_bytes=64)
+            wsc = sb.tile([P, NQ], U8, name=f"wsc{e}", align_bytes=64)
+            nc.vector.quantize_mx(out=wq[:].bitcast(FP8X4), scales=wsc[:], in_=w[:].rearrange("p q t -> p (q t)"))
+            for c in range(2):
+                vc = slice(e * DV + c * (DV // 2), e * DV + (c + 1) * (DV // 2))
+                nc.tensor.matmul_mx(
+                    out=acc[c][:],
+                    lhsT=wq[:].bitcast(FP8X4),
+                    lhsT_scale=wsc[:],
+                    rhs=vg[:, vc].bitcast(FP8X4),
+                    rhs_scale=vscg[V_PLANE:P, vc],
+                    start=(e == 0),
+                    stop=(e == PAGES - 1),
+                )
+
+        y0 = sb.tile([P, DV // 2], F32, name="y0")
+        y1 = sb.tile([P, DV // 2], F32, name="y1")
+        nc.vector.tensor_scalar(y0[:], acc[0][:], 1.0 / 16.0, None, ALU.mult)
+        nc.sync.dma_start(out[0, :, 0 : DV // 2], y0[:])
+        nc.scalar.activation(y1[:], acc[1][:], ACT.Copy, scale=1.0 / 16.0)
+        nc.scalar.dma_start(out[0, :, DV // 2 : DV], y1[:])

@@ -43,90 +43,96 @@ def tile_attend_pkv8q_sigm_cap_kernel(
         ks = sb.tile([P, POOL], U8, name="ks")
         vw = sb.tile([P, POOL_PAGES * DV], I32, name="vw")
         vsc = sb.tile([P, POOL_PAGES * DV], U8, name="vsc")
-        vst = sb.tile([P, POOL], F32, name="vst")
+        vst = sb.tile([P, POOL], F32, name="vst", tag="vst")
         qw = sb.tile([P, NQ], I32, name="qw", align_bytes=64)
         qs = sb.tile([P, NQ], U8, name="qs", align_bytes=64)
-        ident = sb.tile([P, P], F32, name="ident")
+        ident = sb.tile([P, P + 8], F32, name="ident")
         warm = sb.tile([P, 1], F32, name="warm")
 
         nc.vector.memset(ks[:].bitcast(I32), 0)
         nc.vector.memset(qs[:].bitcast(I32), 0)
-        nc.vector.memset(vsc[:].bitcast(I32), 0)
+        nc.vector.memset(ident[:], 0.0)
         nc.vector.memset(vst[0:VS_ROW, :], 0.0)
+        nc.vector.memset(vsc[:].bitcast(I32), 0)
         nc.sync.dma_start(offs_t[:], offs)
-        nc.sync.dma_start(vst[VS_ROW : VS_ROW + 1, :], vs[0:1, :])
-        nc.sync.dma_start(qw[:], q_words[0, 0].rearrange("p n t -> p (n t)").bitcast(I32))
+        nc.sync.dma_start(voffs_t[:], voffs)
+        nc.scalar.dma_start(vst[VS_ROW : VS_ROW + 1, :], vs[0:1, :])
         for r in range(4):
             nc.sync.dma_start(ks[r:P:32, :].bitcast(I32), k_scales[0, r:16:4, :].bitcast(I32))
-        nc.scalar.dma_start(kw[:], k_words[0].rearrange("p n t -> p (n t)").bitcast(I32))
-        nc.sync.dma_start(voffs_t[:], voffs)
+        nc.scalar.dma_start(kw[:], k_words[0].rearrange("p n t -> p (n t)").bitcast(I32), max_dma_last_dim=4096)
+        nc.sync.dma_start(qw[:], q_words[0, 0].rearrange("p n t -> p (n t)").bitcast(I32))
         for r in range(4):
             nc.sync.dma_start(qs[r:P:32, :].bitcast(I32), q_scales[0, 0, r:16:4, :].bitcast(I32))
-        make_identity(nc, ident[:])
-        nc.scalar.activation(warm[:], ident[:, 0:1], ACT.Tanh)
+        nc.scalar.activation(warm[:], ident[:, P : P + 1], ACT.Tanh)
         nc.scalar.dma_start(
             vw[:].rearrange("p (u e) -> p u e", u=POOL_PAGES),
             v_words.rearrange("u p e t -> p u (e t)").bitcast(I32),
         )
+        make_identity(nc, ident[:, 0:P], nomemset=True)
         for r in range(4):
             nc.gpsimd.dma_start(
                 vsc[V_PLANE + r : P : 32, :].bitcast(I32).rearrange("p (u c) -> p u c", u=POOL_PAGES),
                 v_scales[:, r:16:4, :].bitcast(I32).rearrange("u g c -> g u c"),
             )
 
-        vsg = sb.tile([P, SLOTS], F32, name="vsg")
-        nc.vector.tensor_copy(vsg[:], vst[:].indirect(offs_t[:]))
+        cols = PAGE // 16
+        page_offs = [offs_t[:, e * cols : (e + 1) * cols] for e in range(PAGES)]
+        vcols = DV // 16
+        page_voffs = [voffs_t[:, e * vcols : (e + 1) * vcols] for e in range(PAGES)]
+
         vs_half = sb.tile([P, PAGES, PACK], F32, name="vs_half")
         for e in range(PAGES):
+            vsg = sb.tile([P, PAGE], F32, name=f"vsg{e}")
+            nc.vector.tensor_copy(vsg[:], vst[:].indirect(page_offs[e]))
             turned = ps.tile([P, PACK, P], F32, name=f"turned{e}")
             for t in range(PACK):
-                nc.tensor.transpose(turned[:, t, :], vsg[:, e * PAGE + t : (e + 1) * PAGE : PACK], ident[:])
+                nc.tensor.transpose(turned[:, t, :], vsg[:, t:PAGE:PACK], ident[:, 0:P])
             nc.scalar.activation(vs_half[:, e, :], turned[:, :, VS_ROW], ACT.Copy, scale=0.5)
 
-        ksg = sb.tile([P, SLOTS], U8, name="ksg")
-        nc.vector.tensor_copy(ksg[:], ks[:].indirect(offs_t[:]))
-        ksp = sb.tile([P, SLOTS], U8, name="ksp", align_bytes=64)
-        nc.vector.tensor_copy(
-            ksp[:].rearrange("k (e t p) -> k e t p", e=PAGES, t=PACK),
-            ksg[:].rearrange("k (e p t) -> k e t p", e=PAGES, t=PACK),
-        )
-
-        cols = PAGE // 16
-        kg = []
+        ksg = sb.tile([P, PAGES, PAGE], U8, name="ksg", tag="vst")
         for e in range(PAGES):
-            g = sb.tile([P, PAGE], U32, name=f"kg{e}", align_bytes=64)
+            nc.vector.tensor_copy(ksg[:, e, :], ks[:].indirect(page_offs[e]))
+
+        kg = []
+        ksp = []
+        for e in range(PAGES):
+            sp = sb.tile([P, PAGE], U8, name=f"ksp{e}", align_bytes=64)
+            nc.vector.tensor_copy(
+                sp[:].rearrange("k (t p) -> k t p", t=PACK),
+                ksg[:, e, :].rearrange("k (p t) -> k t p", t=PACK),
+            )
+            g = sb.tile([P, PAGE], U32, name=f"kg{e}", tag=f"kg{e}", align_bytes=64)
             nc.vector.tensor_copy(
                 g[:].rearrange("k (t p) -> k p t", t=PACK),
-                kw[:].bitcast(U32).indirect(offs_t[:, e * cols : (e + 1) * cols]),
+                kw[:].bitcast(U32).indirect(page_offs[e]),
             )
             kg.append(g)
+            ksp.append(sp)
 
-        vscg = sb.tile([P, PAGES * DV], U8, name="vscg", align_bytes=64)
-        nc.vector.tensor_copy(vscg[:], vsc[:].indirect(voffs_t[:]))
-
-        p2 = []
+        th = []
         for e in range(PAGES):
             score = ps.tile([P, PACK, NQ], F32, name=f"score{e}")
             for t in range(PACK):
                 nc.tensor.matmul_mx(
                     out=score[:, t, :],
                     lhsT=kg[e][:, t * P : (t + 1) * P].bitcast(FP8X4),
-                    lhsT_scale=ksp[:, e * PAGE + t * P : e * PAGE + (t + 1) * P],
+                    lhsT_scale=ksp[e][:, t * P : (t + 1) * P],
                     rhs=qw[:].bitcast(FP8X4),
                     rhs_scale=qs[:],
                     start=True,
                     stop=True,
                 )
-            half_cap = sb.tile([P, NQ, PACK], F32, name=f"half_cap{e}")
+            half_cap = sb.tile([P, NQ, PACK], F32, name=f"half_cap{e}", tag=f"half_cap{e}", align_bytes=64)
             nc.scalar.activation(half_cap[:], score[:].rearrange("p t q -> p q t"), ACT.Tanh, scale=0.5)
-            th = sb.tile([P, NQ, PACK], F32, name=f"th{e}")
-            pieces = 2
-            step = NQ // pieces
-            for h in range(pieces):
-                nc.scalar.activation(th[:, h * step : (h + 1) * step, :], half_cap[:, h * step : (h + 1) * step, :], ACT.Tanh)
-            p2.append(th)
+            th_e = sb.tile([P, NQ, PACK], F32, name=f"th{e}")
+            for h in range(2):
+                qh = slice(h * (NQ // 2), (h + 1) * (NQ // 2))
+                nc.scalar.activation(th_e[:, qh, :], half_cap[:, qh, :], ACT.Tanh)
+            th.append(th_e)
 
-        vg = sb.tile([P, PAGES * DV], U32, name="vg", align_bytes=64)
+        vscg = sb.tile([P, PAGES * DV], U8, name="vscg", tag="kg0", align_bytes=64)
+        nc.vector.tensor_copy(vscg[:], vsc[:].indirect(voffs_t[:]))
+
         acc = [ps.tile([P, DV // 2], F32, name=f"acc{c}") for c in range(2)]
         for e in range(PAGES):
             w = sb.tile([P, NQ, PACK], BF16, name=f"w{e}", align_bytes=64)
@@ -134,25 +140,25 @@ def tile_attend_pkv8q_sigm_cap_kernel(
                 qh = slice(h * (NQ // 2), (h + 1) * (NQ // 2))
                 nc.vector.scalar_tensor_tensor(
                     out=w[:, qh, :],
-                    in0=p2[e][:, qh, :],
+                    in0=th[e][:, qh, :],
                     scalar=1.0,
                     in1=vs_half[:, e, :].unsqueeze(1).to_broadcast([P, NQ // 2, PACK]),
                     op0=ALU.add,
                     op1=ALU.mult,
                 )
-            if e == 0:
-                nc.vector.tensor_copy(vg[:], vw[:].bitcast(U32).indirect(voffs_t[:]))
+            vg = sb.tile([P, DV], U32, name=f"vg{e}", tag=f"half_cap{e}", align_bytes=64)
+            nc.vector.tensor_copy(vg[:], vw[:].bitcast(U32).indirect(page_voffs[e]))
             wq = sb.tile([P, NQ], U32, name=f"wq{e}", align_bytes=64)
             wsc = sb.tile([P, NQ], U8, name=f"wsc{e}", align_bytes=64)
             nc.vector.quantize_mx(out=wq[:].bitcast(FP8X4), scales=wsc[:], in_=w[:].rearrange("p q t -> p (q t)"))
             for c in range(2):
-                vc = slice(e * DV + c * (DV // 2), e * DV + (c + 1) * (DV // 2))
+                vc = slice(c * (DV // 2), (c + 1) * (DV // 2))
                 nc.tensor.matmul_mx(
                     out=acc[c][:],
                     lhsT=wq[:].bitcast(FP8X4),
                     lhsT_scale=wsc[:],
                     rhs=vg[:, vc].bitcast(FP8X4),
-                    rhs_scale=vscg[V_PLANE:P, vc],
+                    rhs_scale=vscg[V_PLANE:P, e * DV + c * (DV // 2) : e * DV + (c + 1) * (DV // 2)],
                     start=(e == 0),
                     stop=(e == PAGES - 1),
                 )

@@ -42,18 +42,16 @@ def tile_attend_pkv8q_sigm_cap_kernel(
         kw = sb.tile([P, POOL], I32, name="kw")
         ks = sb.tile([P, POOL], U8, name="ks")
         vw = sb.tile([P, POOL_PAGES * DV], I32, name="vw")
-        vsc = sb.tile([P, POOL_PAGES * DV], U8, name="vsc")
-        vst = sb.tile([P, POOL], F32, name="vst", tag="vst")
+        vst = sb.tile([P, POOL], F32, name="vst")
         qw = sb.tile([P, NQ], I32, name="qw", align_bytes=64)
         qs = sb.tile([P, NQ], U8, name="qs", align_bytes=64)
         ident = sb.tile([P, P + 8], F32, name="ident")
-        warm = sb.tile([P, 1], F32, name="warm")
+        warm = sb.tile([P, 1], F32, name="warm", tag="warm")
 
         nc.vector.memset(ks[:].bitcast(I32), 0)
         nc.vector.memset(qs[:].bitcast(I32), 0)
         nc.vector.memset(ident[:], 0.0)
         nc.vector.memset(vst[0:VS_ROW, :], 0.0)
-        nc.vector.memset(vsc[:].bitcast(I32), 0)
         nc.sync.dma_start(offs_t[:], offs)
         nc.sync.dma_start(voffs_t[:], voffs)
         nc.scalar.dma_start(vst[VS_ROW : VS_ROW + 1, :], vs[0:1, :])
@@ -69,16 +67,17 @@ def tile_attend_pkv8q_sigm_cap_kernel(
             v_words.rearrange("u p e t -> p u (e t)").bitcast(I32),
         )
         make_identity(nc, ident[:, 0:P], nomemset=True)
+        vsc = sb.tile([P, POOL_PAGES * DV], U8, name="vsc", tag="warm")
+        nc.gpsimd.memset(vsc[:].bitcast(I32), 0)
         for r in range(4):
-            nc.gpsimd.dma_start(
+            nc.scalar.dma_start(
                 vsc[V_PLANE + r : P : 32, :].bitcast(I32).rearrange("p (u c) -> p u c", u=POOL_PAGES),
                 v_scales[:, r:16:4, :].bitcast(I32).rearrange("u g c -> g u c"),
             )
 
+
         cols = PAGE // 16
         page_offs = [offs_t[:, e * cols : (e + 1) * cols] for e in range(PAGES)]
-        vcols = DV // 16
-        page_voffs = [voffs_t[:, e * vcols : (e + 1) * vcols] for e in range(PAGES)]
 
         vs_half = sb.tile([P, PAGES, PACK], F32, name="vs_half")
         for e in range(PAGES):
@@ -89,76 +88,75 @@ def tile_attend_pkv8q_sigm_cap_kernel(
                 nc.tensor.transpose(turned[:, t, :], vsg[:, t:PAGE:PACK], ident[:, 0:P])
             nc.scalar.activation(vs_half[:, e, :], turned[:, :, VS_ROW], ACT.Copy, scale=0.5)
 
-        ksg = sb.tile([P, PAGES, PAGE], U8, name="ksg", tag="vst")
+        ksg = sb.tile([P, PAGES, PAGE], U8, name="ksg", align_bytes=64)
         for e in range(PAGES):
             nc.vector.tensor_copy(ksg[:, e, :], ks[:].indirect(page_offs[e]))
 
         kg = []
-        ksp = []
         for e in range(PAGES):
-            sp = sb.tile([P, PAGE], U8, name=f"ksp{e}", align_bytes=64)
-            nc.vector.tensor_copy(
-                sp[:].rearrange("k (t p) -> k t p", t=PACK),
-                ksg[:, e, :].rearrange("k (p t) -> k t p", t=PACK),
-            )
-            g = sb.tile([P, PAGE], U32, name=f"kg{e}", tag=f"kg{e}", align_bytes=64)
-            nc.vector.tensor_copy(
-                g[:].rearrange("k (t p) -> k p t", t=PACK),
-                kw[:].bitcast(U32).indirect(page_offs[e]),
-            )
+            g = sb.tile([P, PAGE], U32, name=f"kg{e}", align_bytes=64)
+            nc.vector.tensor_copy(g[:], kw[:].bitcast(U32).indirect(page_offs[e]))
             kg.append(g)
-            ksp.append(sp)
 
+        half_caps = []
+        for e in range(PAGES):
+            score = ps.tile([P, PAGE], F32, name=f"score{e}")
+            nc.tensor.matmul_mx(
+                out=score[:],
+                lhsT=qw[:].bitcast(FP8X4),
+                lhsT_scale=qs[:],
+                rhs=kg[e][:].bitcast(FP8X4),
+                rhs_scale=ksg[:, e, :],
+                start=True,
+                stop=True,
+            )
+            half_cap = sb.tile([P, PACK, P], F32, name=f"half_cap{e}")
+            nc.scalar.activation(half_cap[:], score[:].rearrange("q (p t) -> q t p", t=PACK), ACT.Tanh, scale=0.5)
+            half_caps.append(half_cap)
+
+        pieces = [[slice(0, NQ)], [slice(0, NQ // 2), slice(NQ // 2, NQ)]]
         th = []
         for e in range(PAGES):
-            score = ps.tile([P, PACK, NQ], F32, name=f"score{e}")
+            flipped = ps.tile([P, PACK, NQ], F32, name=f"flipped{e}")
             for t in range(PACK):
-                nc.tensor.matmul_mx(
-                    out=score[:, t, :],
-                    lhsT=kg[e][:, t * P : (t + 1) * P].bitcast(FP8X4),
-                    lhsT_scale=ksp[e][:, t * P : (t + 1) * P],
-                    rhs=qw[:].bitcast(FP8X4),
-                    rhs_scale=qs[:],
-                    start=True,
-                    stop=True,
-                )
-            half_cap = sb.tile([P, NQ, PACK], F32, name=f"half_cap{e}", tag=f"half_cap{e}", align_bytes=64)
-            nc.scalar.activation(half_cap[:], score[:].rearrange("p t q -> p q t"), ACT.Tanh, scale=0.5)
+                nc.tensor.transpose(flipped[:, t, :], half_caps[e][:, t, :], ident[:, 0:P])
             th_e = sb.tile([P, NQ, PACK], F32, name=f"th{e}")
-            for h in range(2):
-                qh = slice(h * (NQ // 2), (h + 1) * (NQ // 2))
-                nc.scalar.activation(th_e[:, qh, :], half_cap[:, qh, :], ACT.Tanh)
+            for qh in pieces[e]:
+                nc.scalar.activation(th_e[:, qh, :], flipped[:, :, qh].rearrange("p t q -> p q t"), ACT.Tanh)
             th.append(th_e)
 
-        vscg = sb.tile([P, PAGES * DV], U8, name="vscg", tag="kg0", align_bytes=64)
+        vg = sb.tile([P, PAGES * DV], U32, name="vg", align_bytes=64)
+        nc.vector.tensor_copy(vg[:], vw[:].bitcast(U32).indirect(voffs_t[:]))
+        vscg = sb.tile([P, PAGES * DV], U8, name="vscg", align_bytes=64)
         nc.vector.tensor_copy(vscg[:], vsc[:].indirect(voffs_t[:]))
 
-        acc = [ps.tile([P, DV // 2], F32, name=f"acc{c}") for c in range(2)]
+        w = []
         for e in range(PAGES):
-            w = sb.tile([P, NQ, PACK], BF16, name=f"w{e}", align_bytes=64)
-            for h in range(2):
-                qh = slice(h * (NQ // 2), (h + 1) * (NQ // 2))
+            w_e = sb.tile([P, NQ, PACK], BF16, name=f"w{e}", align_bytes=64)
+            for qh in pieces[e]:
                 nc.vector.scalar_tensor_tensor(
-                    out=w[:, qh, :],
+                    out=w_e[:, qh, :],
                     in0=th[e][:, qh, :],
                     scalar=1.0,
-                    in1=vs_half[:, e, :].unsqueeze(1).to_broadcast([P, NQ // 2, PACK]),
+                    in1=vs_half[:, e, :].unsqueeze(1).to_broadcast([P, qh.stop - qh.start, PACK]),
                     op0=ALU.add,
                     op1=ALU.mult,
                 )
-            vg = sb.tile([P, DV], U32, name=f"vg{e}", tag=f"half_cap{e}", align_bytes=64)
-            nc.vector.tensor_copy(vg[:], vw[:].bitcast(U32).indirect(page_voffs[e]))
+            w.append(w_e)
+
+        acc = [ps.tile([P, DV // 2], F32, name=f"acc{c}") for c in range(2)]
+        for e in range(PAGES):
             wq = sb.tile([P, NQ], U32, name=f"wq{e}", align_bytes=64)
             wsc = sb.tile([P, NQ], U8, name=f"wsc{e}", align_bytes=64)
-            nc.vector.quantize_mx(out=wq[:].bitcast(FP8X4), scales=wsc[:], in_=w[:].rearrange("p q t -> p (q t)"))
+            nc.vector.quantize_mx(out=wq[:].bitcast(FP8X4), scales=wsc[:], in_=w[e][:].rearrange("p q t -> p (q t)"))
             for c in range(2):
-                vc = slice(c * (DV // 2), (c + 1) * (DV // 2))
+                vc = slice(e * DV + c * (DV // 2), e * DV + (c + 1) * (DV // 2))
                 nc.tensor.matmul_mx(
                     out=acc[c][:],
                     lhsT=wq[:].bitcast(FP8X4),
                     lhsT_scale=wsc[:],
                     rhs=vg[:, vc].bitcast(FP8X4),
-                    rhs_scale=vscg[V_PLANE:P, e * DV + c * (DV // 2) : e * DV + (c + 1) * (DV // 2)],
+                    rhs_scale=vscg[V_PLANE:P, vc],
                     start=(e == 0),
                     stop=(e == PAGES - 1),
                 )

@@ -46,12 +46,14 @@ def tile_attend_pkv8q_sigm_cap_kernel(
         qw = sb.tile([P, NQ], I32, name="qw", align_bytes=64)
         qs = sb.tile([P, NQ], U8, name="qs", align_bytes=64)
         ident = sb.tile([P, P + 8], F32, name="ident")
-        warm = sb.tile([P, 1], F32, name="warm", tag="warm")
+        warm = sb.tile([P, 1], F32, name="warm")
+        vsc = sb.tile([P, POOL_PAGES * DV], U8, name="vsc", tag="vsc", align_bytes=64)
 
         nc.vector.memset(ks[:].bitcast(I32), 0)
         nc.vector.memset(qs[:].bitcast(I32), 0)
         nc.vector.memset(ident[:], 0.0)
-        nc.vector.memset(vst[0:VS_ROW, :], 0.0)
+        nc.vector.memset(vsc[:].bitcast(I32), 0)
+        nc.vector.memset(vst[0:VS_ROW, :].bitcast(I32), 0)
         nc.sync.dma_start(offs_t[:], offs)
         nc.sync.dma_start(voffs_t[:], voffs)
         nc.scalar.dma_start(vst[VS_ROW : VS_ROW + 1, :], vs[0:1, :])
@@ -67,8 +69,6 @@ def tile_attend_pkv8q_sigm_cap_kernel(
             v_words.rearrange("u p e t -> p u (e t)").bitcast(I32),
         )
         make_identity(nc, ident[:, 0:P], nomemset=True)
-        vsc = sb.tile([P, POOL_PAGES * DV], U8, name="vsc", tag="warm")
-        nc.gpsimd.memset(vsc[:].bitcast(I32), 0)
         for r in range(4):
             nc.scalar.dma_start(
                 vsc[V_PLANE + r : P : 32, :].bitcast(I32).rearrange("p (u c) -> p u c", u=POOL_PAGES),
@@ -79,18 +79,17 @@ def tile_attend_pkv8q_sigm_cap_kernel(
         cols = PAGE // 16
         page_offs = [offs_t[:, e * cols : (e + 1) * cols] for e in range(PAGES)]
 
-        vs_half = sb.tile([P, PAGES, PACK], F32, name="vs_half")
+        vs_half = [sb.tile([P, PACK], F32, name=f"vs_half{e}", tag=f"vs_half{e}", align_bytes=64) for e in range(PAGES)]
         for e in range(PAGES):
             vsg = sb.tile([P, PAGE], F32, name=f"vsg{e}")
             nc.vector.tensor_copy(vsg[:], vst[:].indirect(page_offs[e]))
             turned = ps.tile([P, PACK, P], F32, name=f"turned{e}")
             for t in range(PACK):
                 nc.tensor.transpose(turned[:, t, :], vsg[:, t:PAGE:PACK], ident[:, 0:P])
-            nc.scalar.activation(vs_half[:, e, :], turned[:, :, VS_ROW], ACT.Copy, scale=0.5)
+            nc.scalar.activation(vs_half[e][:], turned[:, :, VS_ROW], ACT.Copy, scale=0.5)
 
         ksg = sb.tile([P, PAGES, PAGE], U8, name="ksg", align_bytes=64)
-        for e in range(PAGES):
-            nc.vector.tensor_copy(ksg[:, e, :], ks[:].indirect(page_offs[e]))
+        nc.vector.tensor_copy(ksg[:].rearrange("p e n -> p (e n)"), ks[:].indirect(offs_t[:]))
 
         kg = []
         for e in range(PAGES):
@@ -98,7 +97,7 @@ def tile_attend_pkv8q_sigm_cap_kernel(
             nc.vector.tensor_copy(g[:], kw[:].bitcast(U32).indirect(page_offs[e]))
             kg.append(g)
 
-        half_caps = []
+        scores = []
         for e in range(PAGES):
             score = ps.tile([P, PAGE], F32, name=f"score{e}")
             nc.tensor.matmul_mx(
@@ -110,20 +109,22 @@ def tile_attend_pkv8q_sigm_cap_kernel(
                 start=True,
                 stop=True,
             )
-            half_cap = sb.tile([P, PACK, P], F32, name=f"half_cap{e}")
-            nc.scalar.activation(half_cap[:], score[:].rearrange("q (p t) -> q t p", t=PACK), ACT.Tanh, scale=0.5)
-            half_caps.append(half_cap)
+            scores.append(score)
 
-        pieces = [[slice(0, NQ)], [slice(0, NQ // 2), slice(NQ // 2, NQ)]]
-        th = []
+        pairs = [slice(0, 2), slice(2, 4)]
+        flipped = []
         for e in range(PAGES):
-            flipped = ps.tile([P, PACK, NQ], F32, name=f"flipped{e}")
+            by_place = scores[e][:].rearrange("q (p t) -> q t p", t=PACK)
+            half_cap = [sb.tile([P, 2, P], F32, name=f"half_cap{e}_{h}") for h in range(2)]
+            th = [sb.tile([P, 2, P], F32, name=f"th{e}_{h}") for h in range(2)]
+            for h in range(2):
+                nc.scalar.activation(half_cap[h][:], by_place[:, pairs[h], :], ACT.Tanh, scale=0.5)
+            for h in range(2):
+                nc.scalar.activation(th[h][:], half_cap[h][:], ACT.Tanh)
+            bank = ps.tile([P, PACK, NQ], F32, name=f"flipped{e}")
             for t in range(PACK):
-                nc.tensor.transpose(flipped[:, t, :], half_caps[e][:, t, :], ident[:, 0:P])
-            th_e = sb.tile([P, NQ, PACK], F32, name=f"th{e}")
-            for qh in pieces[e]:
-                nc.scalar.activation(th_e[:, qh, :], flipped[:, :, qh].rearrange("p t q -> p q t"), ACT.Tanh)
-            th.append(th_e)
+                nc.tensor.transpose(bank[:, t, :], th[t // 2][:, t % 2, :], ident[:, 0:P])
+            flipped.append(bank)
 
         vg = sb.tile([P, PAGES * DV], U32, name="vg", align_bytes=64)
         nc.vector.tensor_copy(vg[:], vw[:].bitcast(U32).indirect(voffs_t[:]))
@@ -132,21 +133,20 @@ def tile_attend_pkv8q_sigm_cap_kernel(
 
         w = []
         for e in range(PAGES):
-            w_e = sb.tile([P, NQ, PACK], BF16, name=f"w{e}", align_bytes=64)
-            for qh in pieces[e]:
-                nc.vector.scalar_tensor_tensor(
-                    out=w_e[:, qh, :],
-                    in0=th[e][:, qh, :],
-                    scalar=1.0,
-                    in1=vs_half[:, e, :].unsqueeze(1).to_broadcast([P, qh.stop - qh.start, PACK]),
-                    op0=ALU.add,
-                    op1=ALU.mult,
-                )
+            w_e = sb.tile([P, NQ, PACK], BF16, name=f"w{e}", tag="vsc" if e == 0 else "w_last", align_bytes=64)
+            nc.vector.scalar_tensor_tensor(
+                out=w_e[:],
+                in0=flipped[e][:].rearrange("p t q -> p q t"),
+                scalar=1.0,
+                in1=vs_half[e][:].unsqueeze(1).to_broadcast([P, NQ, PACK]),
+                op0=ALU.add,
+                op1=ALU.mult,
+            )
             w.append(w_e)
 
         acc = [ps.tile([P, DV // 2], F32, name=f"acc{c}") for c in range(2)]
         for e in range(PAGES):
-            wq = sb.tile([P, NQ], U32, name=f"wq{e}", align_bytes=64)
+            wq = sb.tile([P, NQ], U32, name=f"wq{e}", tag="vs_half1" if e == 0 else "wq_last", align_bytes=64)
             wsc = sb.tile([P, NQ], U8, name=f"wsc{e}", align_bytes=64)
             nc.vector.quantize_mx(out=wq[:].bitcast(FP8X4), scales=wsc[:], in_=w[e][:].rearrange("p q t -> p (q t)"))
             for c in range(2):

@@ -47,13 +47,16 @@ def tile_attend_pkv8q_sigm_cap_kernel(
         qs = sb.tile([P, NQ], U8, name="qs", align_bytes=64)
         ident = sb.tile([P, P + 8], F32, name="ident")
         warm = sb.tile([P, 1], F32, name="warm")
+        warm_in = sb.tile([P, 1], F32, name="warm_in")
         vsc = sb.tile([P, POOL_PAGES * DV], U8, name="vsc", tag="vsc", align_bytes=64)
 
-        nc.vector.memset(ks[:].bitcast(I32), 0)
-        nc.vector.memset(qs[:].bitcast(I32), 0)
-        nc.vector.memset(ident[:], 0.0)
-        nc.vector.memset(vsc[:].bitcast(I32), 0)
-        nc.vector.memset(vst[0:VS_ROW, :].bitcast(I32), 0)
+        nc.gpsimd.memset(ks[:].bitcast(I32), 0)
+        nc.vector.memset(warm_in[:], 0.0)
+        nc.vector.memset(vst[0:VS_ROW, 0:1281].bitcast(I32), 0)
+        nc.vector.memset(vst[0:VS_ROW, 1281:2560].bitcast(I32), 0)
+        nc.gpsimd.memset(vst[0:VS_ROW, 2560:POOL].bitcast(I32), 0)
+        nc.gpsimd.memset(qs[:].bitcast(I32), 0)
+        nc.gpsimd.memset(ident[:], 0.0)
         nc.sync.dma_start(offs_t[:], offs)
         nc.sync.dma_start(voffs_t[:], voffs)
         nc.scalar.dma_start(vst[VS_ROW : VS_ROW + 1, :], vs[0:1, :])
@@ -63,12 +66,13 @@ def tile_attend_pkv8q_sigm_cap_kernel(
         nc.sync.dma_start(qw[:], q_words[0, 0].rearrange("p n t -> p (n t)").bitcast(I32))
         for r in range(4):
             nc.sync.dma_start(qs[r:P:32, :].bitcast(I32), q_scales[0, 0, r:16:4, :].bitcast(I32))
-        nc.scalar.activation(warm[:], ident[:, P : P + 1], ACT.Tanh)
+        nc.scalar.activation(warm[:], warm_in[:], ACT.Tanh)
         nc.scalar.dma_start(
             vw[:].rearrange("p (u e) -> p u e", u=POOL_PAGES),
             v_words.rearrange("u p e t -> p u (e t)").bitcast(I32),
         )
         make_identity(nc, ident[:, 0:P], nomemset=True)
+        nc.gpsimd.memset(vsc[:].bitcast(I32), 0)
         for r in range(4):
             nc.scalar.dma_start(
                 vsc[V_PLANE + r : P : 32, :].bitcast(I32).rearrange("p (u c) -> p u c", u=POOL_PAGES),

@@ -101,33 +101,38 @@ def tile_attend_pkv8q_sigm_cap_kernel(
             nc.vector.tensor_copy(g[:], kw[:].bitcast(U32).indirect(page_offs[e]))
             kg.append(g)
 
+        half = PAGE // 2
         scores = []
         for e in range(PAGES):
-            score = ps.tile([P, PAGE], F32, name=f"score{e}")
-            nc.tensor.matmul_mx(
-                out=score[:],
-                lhsT=qw[:].bitcast(FP8X4),
-                lhsT_scale=qs[:],
-                rhs=kg[e][:].bitcast(FP8X4),
-                rhs_scale=ksg[:, e, :],
-                start=True,
-                stop=True,
-            )
-            scores.append(score)
+            banks = [ps.tile([P, half], F32, name=f"score{e}_{h}", tag=f"score{h}") for h in range(2)]
+            for h in range(2):
+                nc.tensor.matmul_mx(
+                    out=banks[h][:],
+                    lhsT=qw[:].bitcast(FP8X4),
+                    lhsT_scale=qs[:],
+                    rhs=kg[e][:, h * half : (h + 1) * half].bitcast(FP8X4),
+                    rhs_scale=ksg[:, e, h * half : (h + 1) * half],
+                    start=True,
+                    stop=True,
+                )
+            half_cap = sb.tile([P, PACK, P], F32, name=f"half_cap{e}")
+            for h in range(2):
+                nc.scalar.activation(
+                    half_cap[:, :, h * (P // 2) : (h + 1) * (P // 2)],
+                    banks[h][:].rearrange("q (p t) -> q t p", t=PACK),
+                    ACT.Tanh,
+                    scale=0.5,
+                )
+            th = sb.tile([P, PACK, P], F32, name=f"th{e}")
+            for places in (slice(0, 2), slice(2, 4)):
+                nc.scalar.activation(th[:, places, :], half_cap[:, places, :], ACT.Tanh)
+            scores.append(th)
 
-        pairs = [slice(0, 2), slice(2, 4)]
         flipped = []
         for e in range(PAGES):
-            by_place = scores[e][:].rearrange("q (p t) -> q t p", t=PACK)
-            half_cap = [sb.tile([P, 2, P], F32, name=f"half_cap{e}_{h}") for h in range(2)]
-            th = [sb.tile([P, 2, P], F32, name=f"th{e}_{h}") for h in range(2)]
-            for h in range(2):
-                nc.scalar.activation(half_cap[h][:], by_place[:, pairs[h], :], ACT.Tanh, scale=0.5)
-            for h in range(2):
-                nc.scalar.activation(th[h][:], half_cap[h][:], ACT.Tanh)
             bank = ps.tile([P, PACK, NQ], F32, name=f"flipped{e}")
             for t in range(PACK):
-                nc.tensor.transpose(bank[:, t, :], th[t // 2][:, t % 2, :], ident[:, 0:P])
+                nc.tensor.transpose(bank[:, t, :], scores[e][:, t, :], ident[:, 0:P])
             flipped.append(bank)
 
         vg = sb.tile([P, PAGES * DV], U32, name="vg", align_bytes=64)
@@ -150,7 +155,7 @@ def tile_attend_pkv8q_sigm_cap_kernel(
 
         acc = [ps.tile([P, DV // 2], F32, name=f"acc{c}") for c in range(2)]
         for e in range(PAGES):
-            wq = sb.tile([P, NQ], U32, name=f"wq{e}", tag="vs_half1" if e == 0 else "wq_last", align_bytes=64)
+            wq = sb.tile([P, NQ], U32, name=f"wq{e}", align_bytes=64)
             wsc = sb.tile([P, NQ], U8, name=f"wsc{e}", align_bytes=64)
             nc.vector.quantize_mx(out=wq[:].bitcast(FP8X4), scales=wsc[:], in_=w[e][:].rearrange("p q t -> p (q t)"))
             for c in range(2):

@@ -25,6 +25,7 @@ DV = 256
 NQ = 128
 VS_ROW = P - 1
 V_PLANE = 4
+K_HEAD = 1024
 FLOPS = 2 * NQ * SLOTS * (D + DV)
 BYTES = (POOL * (D + DV) + NQ * D) * 33 // 32 + POOL * 4 + P * (SLOTS + PAGES * DV) // 8 + NQ * DV * 4
 
@@ -50,35 +51,39 @@ def tile_attend_pkv8q_sigm_cap_kernel(
         warm_in = sb.tile([P, 1], F32, name="warm_in")
         vsc = sb.tile([P, POOL_PAGES * DV], U8, name="vsc", tag="vsc", align_bytes=64)
 
-        nc.gpsimd.memset(ks[:].bitcast(I32), 0)
+        ks_words = ks[:].bitcast(I32)
+        nc.vector.memset(ks_words[:, 0:255], 0)
+        nc.vector.memset(ks_words[:, 255:512], 0)
+        nc.gpsimd.memset(ks_words[:, 512:1024], 0)
         nc.vector.memset(warm_in[:], 0.0)
-        nc.vector.memset(vst[0:VS_ROW, 0:1281].bitcast(I32), 0)
-        nc.vector.memset(vst[0:VS_ROW, 1281:2560].bitcast(I32), 0)
-        nc.gpsimd.memset(vst[0:VS_ROW, 2560:POOL].bitcast(I32), 0)
+        nc.vector.memset(vst[0:VS_ROW, 0:1025].bitcast(I32), 0)
+        nc.vector.memset(vst[0:VS_ROW, 1025:2048].bitcast(I32), 0)
+        nc.gpsimd.memset(vst[0:VS_ROW, 2048:POOL].bitcast(I32), 0)
         nc.gpsimd.memset(qs[:].bitcast(I32), 0)
         nc.gpsimd.memset(ident[:], 0.0)
+        make_identity(nc, ident[:, 0:P], nomemset=True)
+        nc.gpsimd.memset(vsc[:].bitcast(I32), 0)
+        k_src = k_words[0].rearrange("p n t -> p (n t)").bitcast(I32)
         nc.sync.dma_start(offs_t[:], offs)
         nc.sync.dma_start(voffs_t[:], voffs)
         nc.scalar.dma_start(vst[VS_ROW : VS_ROW + 1, :], vs[0:1, :])
+        nc.scalar.dma_start(kw[:, 0:K_HEAD], k_src[:, 0:K_HEAD])
         for r in range(4):
             nc.sync.dma_start(ks[r:P:32, :].bitcast(I32), k_scales[0, r:16:4, :].bitcast(I32))
-        nc.scalar.dma_start(kw[:], k_words[0].rearrange("p n t -> p (n t)").bitcast(I32), max_dma_last_dim=4096)
-        nc.sync.dma_start(qw[:], q_words[0, 0].rearrange("p n t -> p (n t)").bitcast(I32))
-        for r in range(4):
-            nc.sync.dma_start(qs[r:P:32, :].bitcast(I32), q_scales[0, 0, r:16:4, :].bitcast(I32))
+        nc.sync.dma_start(kw[:, K_HEAD:POOL], k_src[:, K_HEAD:POOL], max_dma_last_dim=4096)
         nc.scalar.activation(warm[:], warm_in[:], ACT.Tanh)
+        nc.scalar.dma_start(qw[:], q_words[0, 0].rearrange("p n t -> p (n t)").bitcast(I32))
+        for r in range(4):
+            nc.scalar.dma_start(qs[r:P:32, :].bitcast(I32), q_scales[0, 0, r:16:4, :].bitcast(I32))
         nc.scalar.dma_start(
             vw[:].rearrange("p (u e) -> p u e", u=POOL_PAGES),
             v_words.rearrange("u p e t -> p u (e t)").bitcast(I32),
         )
-        make_identity(nc, ident[:, 0:P], nomemset=True)
-        nc.gpsimd.memset(vsc[:].bitcast(I32), 0)
         for r in range(4):
             nc.scalar.dma_start(
                 vsc[V_PLANE + r : P : 32, :].bitcast(I32).rearrange("p (u c) -> p u c", u=POOL_PAGES),
                 v_scales[:, r:16:4, :].bitcast(I32).rearrange("u g c -> g u c"),
             )
-
 
         cols = PAGE // 16
         page_offs = [offs_t[:, e * cols : (e + 1) * cols] for e in range(PAGES)]
@@ -140,11 +145,12 @@ def tile_attend_pkv8q_sigm_cap_kernel(
         vscg = sb.tile([P, PAGES * DV], U8, name="vscg", align_bytes=64)
         nc.vector.tensor_copy(vscg[:], vsc[:].indirect(voffs_t[:]))
 
+        w_all = sb.tile([P, PAGES, NQ, PACK], BF16, name="w_all", tag="vsc", align_bytes=64)
         w = []
         for e in range(PAGES):
-            w_e = sb.tile([P, NQ, PACK], BF16, name=f"w{e}", tag="vsc" if e == 0 else "w_last", align_bytes=64)
+            w_e = w_all[:, e]
             nc.vector.scalar_tensor_tensor(
-                out=w_e[:],
+                out=w_e,
                 in0=flipped[e][:].rearrange("p t q -> p q t"),
                 scalar=1.0,
                 in1=vs_half[e][:].unsqueeze(1).to_broadcast([P, NQ, PACK]),
@@ -157,7 +163,7 @@ def tile_attend_pkv8q_sigm_cap_kernel(
         for e in range(PAGES):
             wq = sb.tile([P, NQ], U32, name=f"wq{e}", align_bytes=64)
             wsc = sb.tile([P, NQ], U8, name=f"wsc{e}", align_bytes=64)
-            nc.vector.quantize_mx(out=wq[:].bitcast(FP8X4), scales=wsc[:], in_=w[e][:].rearrange("p q t -> p (q t)"))
+            nc.vector.quantize_mx(out=wq[:].bitcast(FP8X4), scales=wsc[:], in_=w[e].rearrange("p q t -> p (q t)"))
             for c in range(2):
                 vc = slice(e * DV + c * (DV // 2), e * DV + (c + 1) * (DV // 2))
                 nc.tensor.matmul_mx(

@@ -56,9 +56,9 @@ def tile_attend_pkv8q_sigm_cap_kernel(
         nc.vector.memset(ks_words[:, 255:512], 0)
         nc.gpsimd.memset(ks_words[:, 512:1024], 0)
         nc.vector.memset(warm_in[:], 0.0)
-        nc.vector.memset(vst[0:VS_ROW, 0:1025].bitcast(I32), 0)
-        nc.vector.memset(vst[0:VS_ROW, 1025:2048].bitcast(I32), 0)
-        nc.gpsimd.memset(vst[0:VS_ROW, 2048:POOL].bitcast(I32), 0)
+        nc.vector.memset(vst[0:VS_ROW, 0:897].bitcast(I32), 0)
+        nc.vector.memset(vst[0:VS_ROW, 897:1792].bitcast(I32), 0)
+        nc.gpsimd.memset(vst[0:VS_ROW, 1792:POOL].bitcast(I32), 0)
         nc.gpsimd.memset(qs[:].bitcast(I32), 0)
         nc.gpsimd.memset(ident[:], 0.0)
         make_identity(nc, ident[:, 0:P], nomemset=True)
@@ -120,7 +120,7 @@ def tile_attend_pkv8q_sigm_cap_kernel(
                     start=True,
                     stop=True,
                 )
-            half_cap = sb.tile([P, PACK, P], F32, name=f"half_cap{e}")
+            half_cap = sb.tile([P, PACK, P], F32, name=f"half_cap{e}", tag="half_cap")
             for h in range(2):
                 nc.scalar.activation(
                     half_cap[:, :, h * (P // 2) : (h + 1) * (P // 2)],
@@ -130,7 +130,9 @@ def tile_attend_pkv8q_sigm_cap_kernel(
                 )
             th = sb.tile([P, PACK, P], F32, name=f"th{e}")
             for places in (slice(0, 2), slice(2, 4)):
-                nc.scalar.activation(th[:, places, :], half_cap[:, places, :], ACT.Tanh)
+                for h in range(2):
+                    rows = slice(h * (P // 2), (h + 1) * (P // 2))
+                    nc.scalar.activation(th[:, places, rows], half_cap[:, places, rows], ACT.Tanh)
             scores.append(th)
 
         flipped = []

@@ -18,6 +18,8 @@ PACK = 4
 PAGE = 512
 PAGES = 2
 SLOTS = PAGE * PAGES
+CHUNK = 256
+CHUNKS = SLOTS // CHUNK
 POOL = 4096
 POOL_PAGES = POOL // PAGE
 D = 512
@@ -25,7 +27,7 @@ DV = 256
 NQ = 128
 VS_ROW = P - 1
 V_PLANE = 4
-K_HEAD = 1024
+VS_SPLIT = 3328
 FLOPS = 2 * NQ * SLOTS * (D + DV)
 BYTES = (POOL * (D + DV) + NQ * D) * 33 // 32 + POOL * 4 + P * (SLOTS + PAGES * DV) // 8 + NQ * DV * 4
 
@@ -46,126 +48,150 @@ def tile_attend_pkv8q_sigm_cap_kernel(
         vst = sb.tile([P, POOL], F32, name="vst")
         qw = sb.tile([P, NQ], I32, name="qw", align_bytes=64)
         qs = sb.tile([P, NQ], U8, name="qs", align_bytes=64)
-        ident = sb.tile([P, P + 8], F32, name="ident")
+        ident = sb.tile([P, P], F32, name="ident")
+        vsc = sb.tile([P, POOL_PAGES * DV], U8, name="vsc", align_bytes=64)
         warm = sb.tile([P, 1], F32, name="warm")
         warm_in = sb.tile([P, 1], F32, name="warm_in")
-        vsc = sb.tile([P, POOL_PAGES * DV], U8, name="vsc", tag="vsc", align_bytes=64)
 
-        ks_words = ks[:].bitcast(I32)
-        nc.vector.memset(ks_words[:, 0:255], 0)
-        nc.vector.memset(ks_words[:, 255:512], 0)
-        nc.gpsimd.memset(ks_words[:, 512:1024], 0)
-        nc.vector.memset(warm_in[:], 0.0)
-        nc.vector.memset(vst[0:VS_ROW, 0:897].bitcast(I32), 0)
-        nc.vector.memset(vst[0:VS_ROW, 897:1792].bitcast(I32), 0)
-        nc.gpsimd.memset(vst[0:VS_ROW, 1792:POOL].bitcast(I32), 0)
-        nc.gpsimd.memset(qs[:].bitcast(I32), 0)
-        nc.gpsimd.memset(ident[:], 0.0)
-        make_identity(nc, ident[:, 0:P], nomemset=True)
-        nc.gpsimd.memset(vsc[:].bitcast(I32), 0)
-        k_src = k_words[0].rearrange("p n t -> p (n t)").bitcast(I32)
-        nc.sync.dma_start(offs_t[:], offs)
-        nc.sync.dma_start(voffs_t[:], voffs)
-        nc.scalar.dma_start(vst[VS_ROW : VS_ROW + 1, :], vs[0:1, :])
-        nc.scalar.dma_start(kw[:, 0:K_HEAD], k_src[:, 0:K_HEAD])
-        for r in range(4):
-            nc.sync.dma_start(ks[r:P:32, :].bitcast(I32), k_scales[0, r:16:4, :].bitcast(I32))
-        nc.sync.dma_start(kw[:, K_HEAD:POOL], k_src[:, K_HEAD:POOL], max_dma_last_dim=4096)
-        nc.scalar.activation(warm[:], warm_in[:], ACT.Tanh)
-        nc.scalar.dma_start(qw[:], q_words[0, 0].rearrange("p n t -> p (n t)").bitcast(I32))
-        for r in range(4):
-            nc.scalar.dma_start(qs[r:P:32, :].bitcast(I32), q_scales[0, 0, r:16:4, :].bitcast(I32))
-        nc.scalar.dma_start(
-            vw[:].rearrange("p (u e) -> p u e", u=POOL_PAGES),
-            v_words.rearrange("u p e t -> p u (e t)").bitcast(I32),
-        )
-        for r in range(4):
-            nc.scalar.dma_start(
+        def fill_odd(view, a, b):
+            m = a + (b - a) // 2 - 1 + ((b - a) // 2) % 2
+            nc.vector.memset(view[:, a:m], 0)
+            nc.vector.memset(view[:, m:b], 0)
+
+        def q_scale_rows(engine, r):
+            engine.dma_start(qs[r:P:32, :].bitcast(I32), q_scales[0, 0, r:16:4, :].bitcast(I32))
+
+        def k_scale_rows(engine, r):
+            engine.dma_start(ks[r:P:32, :].bitcast(I32), k_scales[0, r:16:4, :].bitcast(I32))
+
+        def v_scale_rows(engine, r):
+            engine.dma_start(
                 vsc[V_PLANE + r : P : 32, :].bitcast(I32).rearrange("p (u c) -> p u c", u=POOL_PAGES),
                 v_scales[:, r:16:4, :].bitcast(I32).rearrange("u g c -> g u c"),
             )
 
-        cols = PAGE // 16
-        page_offs = [offs_t[:, e * cols : (e + 1) * cols] for e in range(PAGES)]
+        def keys(engine, a, b):
+            engine.dma_start(kw[:, a:b], k_src[:, a:b], max_dma_last_dim=4096)
 
-        vs_half = [sb.tile([P, PACK], F32, name=f"vs_half{e}", tag=f"vs_half{e}", align_bytes=64) for e in range(PAGES)]
+        k_src = k_words[0].rearrange("p n t -> p (n t)").bitcast(I32)
+        ks_words = ks[:].bitcast(I32)
+        vs_words = vst[0:VS_ROW, :].bitcast(I32)
+        fill_odd(ks_words, 0, 512)
+        nc.gpsimd.memset(ks_words[:, 512:1024], 0)
+        nc.gpsimd.memset(warm_in[:], 0.0)
+        nc.gpsimd.memset(qs[:].bitcast(I32), 0)
+        make_identity(nc, ident[:])
+        for r in range(1, 4):
+            q_scale_rows(nc.gpsimd, r)
+        fill_odd(vsc[:].bitcast(I32), 0, 512)
+        fill_odd(vs_words, 0, VS_SPLIT)
+        nc.gpsimd.memset(vs_words[:, VS_SPLIT:POOL], 0)
+
+        nc.sync.dma_start(offs_t[:], offs)
+        nc.sync.dma_start(voffs_t[:], voffs)
+        nc.scalar.dma_start(vst[VS_ROW : VS_ROW + 1, :], vs[0:1, :])
+        keys(nc.scalar, 0, 1024)
+        nc.scalar.activation(warm[:], warm_in[:], ACT.Tanh)
+        for r in range(4):
+            k_scale_rows(nc.sync, r)
+        keys(nc.sync, 1024, 4096)
+        for r in range(4):
+            v_scale_rows(nc.scalar, r)
+        nc.sync.dma_start(qw[:], q_words[0, 0].rearrange("p n t -> p (n t)").bitcast(I32))
+        q_scale_rows(nc.sync, 0)
+        nc.sync.dma_start(
+            vw[:].rearrange("p (u e) -> p u e", u=POOL_PAGES),
+            v_words.rearrange("u p e t -> p u (e t)").bitcast(I32),
+        )
+
+        page_cols = PAGE // 16
+        chunk_cols = CHUNK // 16
+
+        turned = []
         for e in range(PAGES):
             vsg = sb.tile([P, PAGE], F32, name=f"vsg{e}")
-            nc.vector.tensor_copy(vsg[:], vst[:].indirect(page_offs[e]))
-            turned = ps.tile([P, PACK, P], F32, name=f"turned{e}")
+            nc.scalar.activation(vsg[:], vst[:].indirect(offs_t[:, e * page_cols : (e + 1) * page_cols]), ACT.Copy)
+            bank = ps.tile([P, PACK, P], F32, name=f"turned{e}", tag=f"bank{e}")
             for t in range(PACK):
-                nc.tensor.transpose(turned[:, t, :], vsg[:, t:PAGE:PACK], ident[:, 0:P])
-            nc.scalar.activation(vs_half[e][:], turned[:, :, VS_ROW], ACT.Copy, scale=0.5)
-
-        ksg = sb.tile([P, PAGES, PAGE], U8, name="ksg", align_bytes=64)
-        nc.vector.tensor_copy(ksg[:].rearrange("p e n -> p (e n)"), ks[:].indirect(offs_t[:]))
-
-        kg = []
+                nc.tensor.transpose(bank[:, t, :], vsg[:, t:PAGE:PACK], ident[:])
+            turned.append(bank)
+        vs_half = [sb.tile([P, PACK], F32, name=f"vs_half{e}", align_bytes=64) for e in range(PAGES)]
         for e in range(PAGES):
-            g = sb.tile([P, PAGE], U32, name=f"kg{e}", align_bytes=64)
-            nc.vector.tensor_copy(g[:], kw[:].bitcast(U32).indirect(page_offs[e]))
-            kg.append(g)
+            nc.scalar.activation(vs_half[e][:], turned[e][:, :, VS_ROW], ACT.Copy, scale=0.5)
 
-        half = PAGE // 2
-        scores = []
-        for e in range(PAGES):
-            banks = [ps.tile([P, half], F32, name=f"score{e}_{h}", tag=f"score{h}") for h in range(2)]
-            for h in range(2):
-                nc.tensor.matmul_mx(
-                    out=banks[h][:],
-                    lhsT=qw[:].bitcast(FP8X4),
-                    lhsT_scale=qs[:],
-                    rhs=kg[e][:, h * half : (h + 1) * half].bitcast(FP8X4),
-                    rhs_scale=ksg[:, e, h * half : (h + 1) * half],
-                    start=True,
-                    stop=True,
-                )
-            half_cap = sb.tile([P, PACK, P], F32, name=f"half_cap{e}", tag="half_cap")
-            for h in range(2):
-                nc.scalar.activation(
-                    half_cap[:, :, h * (P // 2) : (h + 1) * (P // 2)],
-                    banks[h][:].rearrange("q (p t) -> q t p", t=PACK),
-                    ACT.Tanh,
-                    scale=0.5,
-                )
-            th = sb.tile([P, PACK, P], F32, name=f"th{e}")
-            for places in (slice(0, 2), slice(2, 4)):
-                for h in range(2):
-                    rows = slice(h * (P // 2), (h + 1) * (P // 2))
-                    nc.scalar.activation(th[:, places, rows], half_cap[:, places, rows], ACT.Tanh)
-            scores.append(th)
-
-        flipped = []
-        for e in range(PAGES):
-            bank = ps.tile([P, PACK, NQ], F32, name=f"flipped{e}")
-            for t in range(PACK):
-                nc.tensor.transpose(bank[:, t, :], scores[e][:, t, :], ident[:, 0:P])
-            flipped.append(bank)
-
-        vg = sb.tile([P, PAGES * DV], U32, name="vg", align_bytes=64)
-        nc.vector.tensor_copy(vg[:], vw[:].bitcast(U32).indirect(voffs_t[:]))
+        ksg = sb.tile([P, SLOTS], U8, name="ksg", align_bytes=64)
+        nc.vector.tensor_copy(ksg[:], ks[:].indirect(offs_t[:]))
         vscg = sb.tile([P, PAGES * DV], U8, name="vscg", align_bytes=64)
         nc.vector.tensor_copy(vscg[:], vsc[:].indirect(voffs_t[:]))
 
-        w_all = sb.tile([P, PAGES, NQ, PACK], BF16, name="w_all", tag="vsc", align_bytes=64)
-        w = []
-        for e in range(PAGES):
-            w_e = w_all[:, e]
+        banks = []
+        for c in range(CHUNKS):
+            g = sb.tile([P, CHUNK], U32, name=f"kg{c}", align_bytes=64)
+            nc.vector.tensor_copy(g[:], kw[:].bitcast(U32).indirect(offs_t[:, c * chunk_cols : (c + 1) * chunk_cols]))
+            bank = ps.tile([P, CHUNK], F32, name=f"score{c}", tag=f"bank{c % 2}")
+            nc.tensor.matmul_mx(
+                out=bank[:],
+                lhsT=qw[:].bitcast(FP8X4),
+                lhsT_scale=qs[:],
+                rhs=g[:].bitcast(FP8X4),
+                rhs_scale=ksg[:, c * CHUNK : (c + 1) * CHUNK],
+                start=True,
+                stop=True,
+            )
+            banks.append(bank)
+
+        rows = CHUNK // PACK
+        half_cap = [sb.tile([P, PACK, rows], F32, name=f"half_cap{c}") for c in range(CHUNKS)]
+        th = [sb.tile([P, PACK, P], F32, name=f"th{e}") for e in range(PAGES)]
+        flipped = [ps.tile([P, PACK, NQ], F32, name=f"flipped{e}") for e in range(PAGES)]
+
+        def cap(c):
+            nc.scalar.activation(
+                half_cap[c][:], banks[c][:].rearrange("q (p t) -> q t p", t=PACK), ACT.Tanh, scale=0.5
+            )
+
+        def squash(c, places):
+            e, h = divmod(c, 2)
+            nc.scalar.activation(th[e][:, places, h * rows : (h + 1) * rows], half_cap[c][:, places, :], ACT.Tanh)
+
+        def turn(e, places):
+            for t in range(places.start, places.stop):
+                nc.tensor.transpose(flipped[e][:, t, :], th[e][:, t, :], ident[:])
+
+        every = slice(0, PACK)
+        cap(0)
+        cap(1)
+        squash(0, every)
+        squash(1, every)
+        turn(0, every)
+        cap(2)
+        cap(3)
+        squash(2, every)
+        for places in (slice(0, 2), slice(2, 4)):
+            squash(3, places)
+            turn(1, places)
+
+        vg = sb.tile([P, PAGES * DV], U32, name="vg", align_bytes=64)
+        acc = [ps.tile([P, DV // 2], F32, name=f"acc{c}") for c in range(2)]
+        w = [sb.tile([P, NQ, PACK], BF16, name=f"w{e}", align_bytes=64) for e in range(PAGES)]
+
+        def weigh(e):
             nc.vector.scalar_tensor_tensor(
-                out=w_e,
+                out=w[e][:],
                 in0=flipped[e][:].rearrange("p t q -> p q t"),
                 scalar=1.0,
                 in1=vs_half[e][:].unsqueeze(1).to_broadcast([P, NQ, PACK]),
                 op0=ALU.add,
                 op1=ALU.mult,
             )
-            w.append(w_e)
 
-        acc = [ps.tile([P, DV // 2], F32, name=f"acc{c}") for c in range(2)]
-        for e in range(PAGES):
+        def gather_values():
+            nc.vector.tensor_copy(vg[:], vw[:].bitcast(U32).indirect(voffs_t[:]))
+
+        def product(e):
             wq = sb.tile([P, NQ], U32, name=f"wq{e}", align_bytes=64)
             wsc = sb.tile([P, NQ], U8, name=f"wsc{e}", align_bytes=64)
-            nc.vector.quantize_mx(out=wq[:].bitcast(FP8X4), scales=wsc[:], in_=w[e].rearrange("p q t -> p (q t)"))
+            nc.vector.quantize_mx(out=wq[:].bitcast(FP8X4), scales=wsc[:], in_=w[e][:].rearrange("p q t -> p (q t)"))
             for c in range(2):
                 vc = slice(e * DV + c * (DV // 2), e * DV + (c + 1) * (DV // 2))
                 nc.tensor.matmul_mx(
@@ -177,6 +203,12 @@ def tile_attend_pkv8q_sigm_cap_kernel(
                     start=(e == 0),
                     stop=(e == PAGES - 1),
                 )
+
+        weigh(0)
+        gather_values()
+        product(0)
+        weigh(1)
+        product(1)
 
         y0 = sb.tile([P, DV // 2], F32, name="y0")
         y1 = sb.tile([P, DV // 2], F32, name="y1")

@@ -27,7 +27,8 @@ DV = 256
 NQ = 128
 VS_ROW = P - 1
 V_PLANE = 4
-VS_SPLIT = 3328
+VS_SPLIT = 1536
+K_HEAD = 1280
 FLOPS = 2 * NQ * SLOTS * (D + DV)
 BYTES = (POOL * (D + DV) + NQ * D) * 33 // 32 + POOL * 4 + P * (SLOTS + PAGES * DV) // 8 + NQ * DV * 4
 
@@ -44,7 +45,7 @@ def tile_attend_pkv8q_sigm_cap_kernel(
         voffs_t = sb.tile([P, PAGES * DV // 16], U16, name="voffs_t")
         kw = sb.tile([P, POOL], I32, name="kw")
         ks = sb.tile([P, POOL], U8, name="ks")
-        vw = sb.tile([P, POOL_PAGES * DV], I32, name="vw")
+        vw = sb.tile([P, POOL_PAGES * DV], I32, name="vw", tag="vw", align_bytes=64)
         vst = sb.tile([P, POOL], F32, name="vst")
         qw = sb.tile([P, NQ], I32, name="qw", align_bytes=64)
         qs = sb.tile([P, NQ], U8, name="qs", align_bytes=64)
@@ -64,41 +65,38 @@ def tile_attend_pkv8q_sigm_cap_kernel(
         def k_scale_rows(engine, r):
             engine.dma_start(ks[r:P:32, :].bitcast(I32), k_scales[0, r:16:4, :].bitcast(I32))
 
-        def v_scale_rows(engine, r):
-            engine.dma_start(
-                vsc[V_PLANE + r : P : 32, :].bitcast(I32).rearrange("p (u c) -> p u c", u=POOL_PAGES),
-                v_scales[:, r:16:4, :].bitcast(I32).rearrange("u g c -> g u c"),
-            )
-
         def keys(engine, a, b):
-            engine.dma_start(kw[:, a:b], k_src[:, a:b], max_dma_last_dim=4096)
+            engine.dma_start(kw[:, a:b], k_src[:, a:b], max_dma_last_dim=5632)
 
         k_src = k_words[0].rearrange("p n t -> p (n t)").bitcast(I32)
         ks_words = ks[:].bitcast(I32)
         vs_words = vst[0:VS_ROW, :].bitcast(I32)
+        vsc_words = vsc[:].bitcast(I32)
+        fill_odd(vsc_words, 0, 256)
+        nc.gpsimd.memset(vsc_words[:, 256:512], 0)
         fill_odd(ks_words, 0, 512)
         nc.gpsimd.memset(ks_words[:, 512:1024], 0)
         nc.gpsimd.memset(warm_in[:], 0.0)
         nc.gpsimd.memset(qs[:].bitcast(I32), 0)
-        make_identity(nc, ident[:])
-        for r in range(1, 4):
-            q_scale_rows(nc.gpsimd, r)
-        fill_odd(vsc[:].bitcast(I32), 0, 512)
         fill_odd(vs_words, 0, VS_SPLIT)
+        make_identity(nc, ident[:])
         nc.gpsimd.memset(vs_words[:, VS_SPLIT:POOL], 0)
 
         nc.sync.dma_start(offs_t[:], offs)
         nc.sync.dma_start(voffs_t[:], voffs)
         nc.scalar.dma_start(vst[VS_ROW : VS_ROW + 1, :], vs[0:1, :])
-        keys(nc.scalar, 0, 1024)
+        keys(nc.scalar, 0, K_HEAD)
         nc.scalar.activation(warm[:], warm_in[:], ACT.Tanh)
+        nc.sync.dma_start(
+            vsc[V_PLANE:P:8, :].bitcast(I32).rearrange("p (u c) -> p u c", u=POOL_PAGES),
+            v_scales.bitcast(I32).rearrange("u f c -> f u c"),
+        )
         for r in range(4):
             k_scale_rows(nc.sync, r)
-        keys(nc.sync, 1024, 4096)
-        for r in range(4):
-            v_scale_rows(nc.scalar, r)
+        keys(nc.sync, K_HEAD, POOL)
         nc.sync.dma_start(qw[:], q_words[0, 0].rearrange("p n t -> p (n t)").bitcast(I32))
-        q_scale_rows(nc.sync, 0)
+        for r in range(4):
+            q_scale_rows(nc.sync, r)
         nc.sync.dma_start(
             vw[:].rearrange("p (u e) -> p u e", u=POOL_PAGES),
             v_words.rearrange("u p e t -> p u (e t)").bitcast(I32),
@@ -119,10 +117,14 @@ def tile_attend_pkv8q_sigm_cap_kernel(
         for e in range(PAGES):
             nc.scalar.activation(vs_half[e][:], turned[e][:, :, VS_ROW], ACT.Copy, scale=0.5)
 
-        ksg = sb.tile([P, SLOTS], U8, name="ksg", align_bytes=64)
-        nc.vector.tensor_copy(ksg[:], ks[:].indirect(offs_t[:]))
         vscg = sb.tile([P, PAGES * DV], U8, name="vscg", align_bytes=64)
         nc.vector.tensor_copy(vscg[:], vsc[:].indirect(voffs_t[:]))
+        ksg = sb.tile([P, SLOTS], U8, name="ksg", align_bytes=64)
+        nc.vector.tensor_copy(ksg[:], ks[:].indirect(offs_t[:]))
+        v_plane = sb.tile([P, PAGES * DV], U8, name="v_plane", align_bytes=64)
+        nc.vector.tensor_copy(v_plane[:].bitcast(I32), vscg[:].bitcast(I32))
+        for r in range(1, 4):
+            nc.sync.dma_start(v_plane[V_PLANE + r : P : 32, :].bitcast(I32), vscg[V_PLANE + 8 * r : P : 32, :].bitcast(I32))
 
         banks = []
         for c in range(CHUNKS):
@@ -173,11 +175,13 @@ def tile_attend_pkv8q_sigm_cap_kernel(
 
         vg = sb.tile([P, PAGES * DV], U32, name="vg", align_bytes=64)
         acc = [ps.tile([P, DV // 2], F32, name=f"acc{c}") for c in range(2)]
-        w = [sb.tile([P, NQ, PACK], BF16, name=f"w{e}", align_bytes=64) for e in range(PAGES)]
+        nc.vector.tensor_copy(vg[:], vw[:].bitcast(U32).indirect(voffs_t[:]))
+        w_all = sb.tile([P, PAGES, NQ, PACK], BF16, name="w_all", tag="vw", align_bytes=64)
+        w = [w_all[:, e] for e in range(PAGES)]
 
         def weigh(e):
             nc.vector.scalar_tensor_tensor(
-                out=w[e][:],
+                out=w[e],
                 in0=flipped[e][:].rearrange("p t q -> p q t"),
                 scalar=1.0,
                 in1=vs_half[e][:].unsqueeze(1).to_broadcast([P, NQ, PACK]),
@@ -185,13 +189,10 @@ def tile_attend_pkv8q_sigm_cap_kernel(
                 op1=ALU.mult,
             )
 
-        def gather_values():
-            nc.vector.tensor_copy(vg[:], vw[:].bitcast(U32).indirect(voffs_t[:]))
-
         def product(e):
             wq = sb.tile([P, NQ], U32, name=f"wq{e}", align_bytes=64)
             wsc = sb.tile([P, NQ], U8, name=f"wsc{e}", align_bytes=64)
-            nc.vector.quantize_mx(out=wq[:].bitcast(FP8X4), scales=wsc[:], in_=w[e][:].rearrange("p q t -> p (q t)"))
+            nc.vector.quantize_mx(out=wq[:].bitcast(FP8X4), scales=wsc[:], in_=w[e].rearrange("p q t -> p (q t)"))
             for c in range(2):
                 vc = slice(e * DV + c * (DV // 2), e * DV + (c + 1) * (DV // 2))
                 nc.tensor.matmul_mx(
@@ -199,16 +200,15 @@ def tile_attend_pkv8q_sigm_cap_kernel(
                     lhsT=wq[:].bitcast(FP8X4),
                     lhsT_scale=wsc[:],
                     rhs=vg[:, vc].bitcast(FP8X4),
-                    rhs_scale=vscg[V_PLANE:P, vc],
+                    rhs_scale=v_plane[V_PLANE:P, vc],
                     start=(e == 0),
                     stop=(e == PAGES - 1),
                 )
 
-        weigh(0)
-        gather_values()
-        product(0)
-        weigh(1)
-        product(1)
+        for e in range(PAGES):
+            weigh(e)
+        for e in range(PAGES):
+            product(e)
 
         y0 = sb.tile([P, DV // 2], F32, name="y0")
         y1 = sb.tile([P, DV // 2], F32, name="y1")

@@ -27,7 +27,7 @@ DV = 256
 NQ = 128
 VS_ROW = P - 1
 V_PLANE = 4
-VS_SPLIT = 1536
+VS_SPLIT = 2240
 K_HEAD = 1280
 FLOPS = 2 * NQ * SLOTS * (D + DV)
 BYTES = (POOL * (D + DV) + NQ * D) * 33 // 32 + POOL * 4 + P * (SLOTS + PAGES * DV) // 8 + NQ * DV * 4
@@ -45,12 +45,11 @@ def tile_attend_pkv8q_sigm_cap_kernel(
         voffs_t = sb.tile([P, PAGES * DV // 16], U16, name="voffs_t")
         kw = sb.tile([P, POOL], I32, name="kw")
         ks = sb.tile([P, POOL], U8, name="ks")
-        vw = sb.tile([P, POOL_PAGES * DV], I32, name="vw", tag="vw", align_bytes=64)
         vst = sb.tile([P, POOL], F32, name="vst")
         qw = sb.tile([P, NQ], I32, name="qw", align_bytes=64)
         qs = sb.tile([P, NQ], U8, name="qs", align_bytes=64)
         ident = sb.tile([P, P], F32, name="ident")
-        vsc = sb.tile([P, POOL_PAGES * DV], U8, name="vsc", align_bytes=64)
+        vsc = sb.tile([P, POOL_PAGES * DV], U8, name="vsc", tag="values", align_bytes=64)
         warm = sb.tile([P, 1], F32, name="warm")
         warm_in = sb.tile([P, 1], F32, name="warm_in")
 
@@ -97,28 +96,32 @@ def tile_attend_pkv8q_sigm_cap_kernel(
         nc.sync.dma_start(qw[:], q_words[0, 0].rearrange("p n t -> p (n t)").bitcast(I32))
         for r in range(4):
             q_scale_rows(nc.sync, r)
-        nc.sync.dma_start(
-            vw[:].rearrange("p (u e) -> p u e", u=POOL_PAGES),
-            v_words.rearrange("u p e t -> p u (e t)").bitcast(I32),
-        )
+
+        vscg = sb.tile([P, PAGES * DV], U8, name="vscg", align_bytes=64)
+        nc.vector.tensor_copy(vscg[:], vsc[:].indirect(voffs_t[:]))
 
         page_cols = PAGE // 16
         chunk_cols = CHUNK // 16
 
-        turned = []
-        for e in range(PAGES):
+        def turn_vs(e):
             vsg = sb.tile([P, PAGE], F32, name=f"vsg{e}")
             nc.scalar.activation(vsg[:], vst[:].indirect(offs_t[:, e * page_cols : (e + 1) * page_cols]), ACT.Copy)
             bank = ps.tile([P, PACK, P], F32, name=f"turned{e}", tag=f"bank{e}")
             for t in range(PACK):
                 nc.tensor.transpose(bank[:, t, :], vsg[:, t:PAGE:PACK], ident[:])
-            turned.append(bank)
+            return bank
+
+        turned = [turn_vs(0)]
+        vw = sb.tile([P, POOL_PAGES * DV], I32, name="vw", tag="values", align_bytes=64)
+        nc.scalar.dma_start(
+            vw[:].rearrange("p (u e) -> p u e", u=POOL_PAGES),
+            v_words.rearrange("u p e t -> p u (e t)").bitcast(I32),
+        )
+        turned.append(turn_vs(1))
         vs_half = [sb.tile([P, PACK], F32, name=f"vs_half{e}", align_bytes=64) for e in range(PAGES)]
         for e in range(PAGES):
             nc.scalar.activation(vs_half[e][:], turned[e][:, :, VS_ROW], ACT.Copy, scale=0.5)
 
-        vscg = sb.tile([P, PAGES * DV], U8, name="vscg", align_bytes=64)
-        nc.vector.tensor_copy(vscg[:], vsc[:].indirect(voffs_t[:]))
         ksg = sb.tile([P, SLOTS], U8, name="ksg", align_bytes=64)
         nc.vector.tensor_copy(ksg[:], ks[:].indirect(offs_t[:]))
         v_plane = sb.tile([P, PAGES * DV], U8, name="v_plane", align_bytes=64)
@@ -176,7 +179,7 @@ def tile_attend_pkv8q_sigm_cap_kernel(
         vg = sb.tile([P, PAGES * DV], U32, name="vg", align_bytes=64)
         acc = [ps.tile([P, DV // 2], F32, name=f"acc{c}") for c in range(2)]
         nc.vector.tensor_copy(vg[:], vw[:].bitcast(U32).indirect(voffs_t[:]))
-        w_all = sb.tile([P, PAGES, NQ, PACK], BF16, name="w_all", tag="vw", align_bytes=64)
+        w_all = sb.tile([P, PAGES, NQ, PACK], BF16, name="w_all", tag="values", align_bytes=64)
         w = [w_all[:, e] for e in range(PAGES)]
 
         def weigh(e):

@@ -28,7 +28,7 @@ NQ = 128
 VS_ROW = P - 1
 V_PLANE = 4
 VS_SPLIT = 2240
-K_HEAD = 1280
+PIECE = 4096
 FLOPS = 2 * NQ * SLOTS * (D + DV)
 BYTES = (POOL * (D + DV) + NQ * D) * 33 // 32 + POOL * 4 + P * (SLOTS + PAGES * DV) // 8 + NQ * DV * 4
 
@@ -39,6 +39,7 @@ def tile_attend_pkv8q_sigm_cap_kernel(
     nc = tc.nc
     with ExitStack() as ctx:
         sb = ctx.enter_context(tc.tile_pool(name="sb", bufs=1))
+        shared = ctx.enter_context(tc.tile_pool(name="shared", bufs=1))
         ps = ctx.enter_context(tc.psum_pool(name="ps", bufs=1))
 
         offs_t = sb.tile([P, SLOTS // 16], U16, name="offs_t")
@@ -46,10 +47,11 @@ def tile_attend_pkv8q_sigm_cap_kernel(
         kw = sb.tile([P, POOL], I32, name="kw")
         ks = sb.tile([P, POOL], U8, name="ks")
         vst = sb.tile([P, POOL], F32, name="vst")
+        vw = sb.tile([P, POOL_PAGES * DV], I32, name="vw")
+        vsc = sb.tile([P, POOL_PAGES * DV], U8, name="vsc")
         qw = sb.tile([P, NQ], I32, name="qw", align_bytes=64)
         qs = sb.tile([P, NQ], U8, name="qs", align_bytes=64)
         ident = sb.tile([P, P], F32, name="ident")
-        vsc = sb.tile([P, POOL_PAGES * DV], U8, name="vsc", tag="values", align_bytes=64)
         warm = sb.tile([P, 1], F32, name="warm")
         warm_in = sb.tile([P, 1], F32, name="warm_in")
 
@@ -58,160 +60,152 @@ def tile_attend_pkv8q_sigm_cap_kernel(
             nc.vector.memset(view[:, a:m], 0)
             nc.vector.memset(view[:, m:b], 0)
 
-        def q_scale_rows(engine, r):
-            engine.dma_start(qs[r:P:32, :].bitcast(I32), q_scales[0, 0, r:16:4, :].bitcast(I32))
-
-        def k_scale_rows(engine, r):
-            engine.dma_start(ks[r:P:32, :].bitcast(I32), k_scales[0, r:16:4, :].bitcast(I32))
-
-        def keys(engine, a, b):
-            engine.dma_start(kw[:, a:b], k_src[:, a:b], max_dma_last_dim=5632)
-
-        k_src = k_words[0].rearrange("p n t -> p (n t)").bitcast(I32)
         ks_words = ks[:].bitcast(I32)
         vs_words = vst[0:VS_ROW, :].bitcast(I32)
         vsc_words = vsc[:].bitcast(I32)
+        nc.gpsimd.memset(warm_in[:], 0.0)
         fill_odd(vsc_words, 0, 256)
         nc.gpsimd.memset(vsc_words[:, 256:512], 0)
         fill_odd(ks_words, 0, 512)
         nc.gpsimd.memset(ks_words[:, 512:1024], 0)
-        nc.gpsimd.memset(warm_in[:], 0.0)
         nc.gpsimd.memset(qs[:].bitcast(I32), 0)
         fill_odd(vs_words, 0, VS_SPLIT)
-        make_identity(nc, ident[:])
         nc.gpsimd.memset(vs_words[:, VS_SPLIT:POOL], 0)
+        make_identity(nc, ident[:])
 
-        nc.sync.dma_start(offs_t[:], offs)
-        nc.sync.dma_start(voffs_t[:], voffs)
         nc.scalar.dma_start(vst[VS_ROW : VS_ROW + 1, :], vs[0:1, :])
-        keys(nc.scalar, 0, K_HEAD)
+        nc.scalar.dma_start(
+            kw[:], k_words[0].rearrange("p n t -> p (n t)").bitcast(I32), max_dma_last_dim=PIECE
+        )
         nc.scalar.activation(warm[:], warm_in[:], ACT.Tanh)
+        nc.sync.dma_start(offs_t[:], offs)
         nc.sync.dma_start(
             vsc[V_PLANE:P:8, :].bitcast(I32).rearrange("p (u c) -> p u c", u=POOL_PAGES),
             v_scales.bitcast(I32).rearrange("u f c -> f u c"),
         )
         for r in range(4):
-            k_scale_rows(nc.sync, r)
-        keys(nc.sync, K_HEAD, POOL)
+            nc.sync.dma_start(ks[r:P:32, :].bitcast(I32), k_scales[0, r:16:4, :].bitcast(I32))
+        nc.sync.dma_start(voffs_t[:], voffs)
         nc.sync.dma_start(qw[:], q_words[0, 0].rearrange("p n t -> p (n t)").bitcast(I32))
         for r in range(4):
-            q_scale_rows(nc.sync, r)
+            nc.sync.dma_start(qs[r:P:32, :].bitcast(I32), q_scales[0, 0, r:16:4, :].bitcast(I32))
 
+        ksg = sb.tile([P, SLOTS], U8, name="ksg", align_bytes=64)
+        nc.vector.tensor_copy(ksg[:], ks[:].indirect(offs_t[:]))
         vscg = sb.tile([P, PAGES * DV], U8, name="vscg", align_bytes=64)
         nc.vector.tensor_copy(vscg[:], vsc[:].indirect(voffs_t[:]))
 
         page_cols = PAGE // 16
         chunk_cols = CHUNK // 16
+        vsg = shared.tile([P, SLOTS], F32, name="vsg", offset=0, align_bytes=64)
+        vs_half = [sb.tile([P, PACK], F32, name=f"vs_half{e}", align_bytes=64) for e in range(PAGES)]
 
-        def turn_vs(e):
-            vsg = sb.tile([P, PAGE], F32, name=f"vsg{e}")
-            nc.scalar.activation(vsg[:], vst[:].indirect(offs_t[:, e * page_cols : (e + 1) * page_cols]), ACT.Copy)
-            bank = ps.tile([P, PACK, P], F32, name=f"turned{e}", tag=f"bank{e}")
-            for t in range(PACK):
-                nc.tensor.transpose(bank[:, t, :], vsg[:, t:PAGE:PACK], ident[:])
-            return bank
+        def gather_vs(e):
+            nc.scalar.activation(
+                vsg[:, e * PAGE : (e + 1) * PAGE],
+                vst[:].indirect(offs_t[:, e * page_cols : (e + 1) * page_cols]),
+                ACT.Copy,
+            )
 
-        turned = [turn_vs(0)]
-        vw = sb.tile([P, POOL_PAGES * DV], I32, name="vw", tag="values", align_bytes=64)
+        gather_vs(0)
+        gather_vs(1)
         nc.scalar.dma_start(
             vw[:].rearrange("p (u e) -> p u e", u=POOL_PAGES),
             v_words.rearrange("u p e t -> p u (e t)").bitcast(I32),
         )
-        turned.append(turn_vs(1))
-        vs_half = [sb.tile([P, PACK], F32, name=f"vs_half{e}", align_bytes=64) for e in range(PAGES)]
         for e in range(PAGES):
-            nc.scalar.activation(vs_half[e][:], turned[e][:, :, VS_ROW], ACT.Copy, scale=0.5)
+            turned = ps.tile([P, PACK, P], F32, name=f"turned{e}", tag=f"bank{e}")
+            for t in range(PACK):
+                nc.tensor.transpose(turned[:, t, :], vsg[:, e * PAGE + t : (e + 1) * PAGE : PACK], ident[:])
+            nc.scalar.activation(vs_half[e][:], turned[:, :, VS_ROW], ACT.Copy, scale=0.5)
 
-        ksg = sb.tile([P, SLOTS], U8, name="ksg", align_bytes=64)
-        nc.vector.tensor_copy(ksg[:], ks[:].indirect(offs_t[:]))
         v_plane = sb.tile([P, PAGES * DV], U8, name="v_plane", align_bytes=64)
-        nc.vector.tensor_copy(v_plane[:].bitcast(I32), vscg[:].bitcast(I32))
-        for r in range(1, 4):
-            nc.sync.dma_start(v_plane[V_PLANE + r : P : 32, :].bitcast(I32), vscg[V_PLANE + 8 * r : P : 32, :].bitcast(I32))
+        nc.gpsimd.memset(v_plane[:].bitcast(I32), 0)
+        for r in range(4):
+            nc.sync.dma_start(
+                v_plane[V_PLANE + r : P : 32, :].bitcast(I32), vscg[V_PLANE + 8 * r : P : 32, :].bitcast(I32)
+            )
 
         banks = []
         for c in range(CHUNKS):
-            g = sb.tile([P, CHUNK], U32, name=f"kg{c}", align_bytes=64)
-            nc.vector.tensor_copy(g[:], kw[:].bitcast(U32).indirect(offs_t[:, c * chunk_cols : (c + 1) * chunk_cols]))
-            bank = ps.tile([P, CHUNK], F32, name=f"score{c}", tag=f"bank{c % 2}")
+            cols = slice(c * CHUNK, (c + 1) * CHUNK)
+            kg = shared.tile([P, CHUNK], U32, name=f"kg{c}", offset=4 * CHUNK * c, align_bytes=64)
+            nc.vector.tensor_copy(
+                kg[:], kw[:].bitcast(U32).indirect(offs_t[:, c * chunk_cols : (c + 1) * chunk_cols])
+            )
+            bank = ps.tile([P, CHUNK], F32, name=f"score{c}")
             nc.tensor.matmul_mx(
                 out=bank[:],
                 lhsT=qw[:].bitcast(FP8X4),
                 lhsT_scale=qs[:],
-                rhs=g[:].bitcast(FP8X4),
-                rhs_scale=ksg[:, c * CHUNK : (c + 1) * CHUNK],
+                rhs=kg[:].bitcast(FP8X4),
+                rhs_scale=ksg[:, cols],
                 start=True,
                 stop=True,
             )
             banks.append(bank)
+        vg = shared.tile([P, PAGES * DV], U32, name="vg", offset=0, align_bytes=64)
+        nc.vector.tensor_copy(vg[:], vw[:].bitcast(U32).indirect(voffs_t[:]))
 
         rows = CHUNK // PACK
-        half_cap = [sb.tile([P, PACK, rows], F32, name=f"half_cap{c}") for c in range(CHUNKS)]
-        th = [sb.tile([P, PACK, P], F32, name=f"th{e}") for e in range(PAGES)]
+        half_cap = [sb.tile([P, PACK, P], F32, name=f"half_cap{e}") for e in range(PAGES)]
         flipped = [ps.tile([P, PACK, NQ], F32, name=f"flipped{e}") for e in range(PAGES)]
-
-        def cap(c):
-            nc.scalar.activation(
-                half_cap[c][:], banks[c][:].rearrange("q (p t) -> q t p", t=PACK), ACT.Tanh, scale=0.5
-            )
-
-        def squash(c, places):
+        for c in range(CHUNKS):
             e, h = divmod(c, 2)
-            nc.scalar.activation(th[e][:, places, h * rows : (h + 1) * rows], half_cap[c][:, places, :], ACT.Tanh)
+            nc.scalar.activation(
+                half_cap[e][:, :, h * rows : (h + 1) * rows],
+                banks[c][:].rearrange("q (p t) -> q t p", t=PACK),
+                ACT.Tanh,
+                scale=0.5,
+            )
+        for e in range(PAGES):
+            for t in range(PACK):
+                nc.tensor.transpose(flipped[e][:, t, :], half_cap[e][:, t, :], ident[:])
 
-        def turn(e, places):
-            for t in range(places.start, places.stop):
-                nc.tensor.transpose(flipped[e][:, t, :], th[e][:, t, :], ident[:])
+        th = [sb.tile([P, NQ, PACK], F32, name=f"th{e}") for e in range(PAGES)]
+        w = [sb.tile([P, NQ, PACK], BF16, name=f"w{e}", align_bytes=64) for e in range(PAGES)]
+        wq = [sb.tile([P, NQ], U32, name=f"wq{e}", align_bytes=64) for e in range(PAGES)]
+        wsc = [sb.tile([P, NQ], U8, name=f"wsc{e}", align_bytes=64) for e in range(PAGES)]
+        acc = [ps.tile([P, DV // 2], F32, name=f"acc{c}", tag=f"bank{c}") for c in range(2)]
 
-        every = slice(0, PACK)
-        cap(0)
-        cap(1)
-        squash(0, every)
-        squash(1, every)
-        turn(0, every)
-        cap(2)
-        cap(3)
-        squash(2, every)
-        for places in (slice(0, 2), slice(2, 4)):
-            squash(3, places)
-            turn(1, places)
-
-        vg = sb.tile([P, PAGES * DV], U32, name="vg", align_bytes=64)
-        acc = [ps.tile([P, DV // 2], F32, name=f"acc{c}") for c in range(2)]
-        nc.vector.tensor_copy(vg[:], vw[:].bitcast(U32).indirect(voffs_t[:]))
-        w_all = sb.tile([P, PAGES, NQ, PACK], BF16, name="w_all", tag="values", align_bytes=64)
-        w = [w_all[:, e] for e in range(PAGES)]
-
-        def weigh(e):
+        def weigh(e, q):
+            nc.scalar.activation(th[e][:, q, :], flipped[e][:, :, q].rearrange("p t q -> p q t"), ACT.Tanh)
             nc.vector.scalar_tensor_tensor(
-                out=w[e],
-                in0=flipped[e][:].rearrange("p t q -> p q t"),
+                out=w[e][:, q, :],
+                in0=th[e][:, q, :],
                 scalar=1.0,
-                in1=vs_half[e][:].unsqueeze(1).to_broadcast([P, NQ, PACK]),
+                in1=vs_half[e][:].unsqueeze(1).to_broadcast([P, q.stop - q.start, PACK]),
                 op0=ALU.add,
                 op1=ALU.mult,
             )
 
+        def quantise(e, q):
+            nc.vector.quantize_mx(
+                out=wq[e][:, q].bitcast(FP8X4), scales=wsc[e][:, q], in_=w[e][:, q, :].rearrange("p q t -> p (q t)")
+            )
+
         def product(e):
-            wq = sb.tile([P, NQ], U32, name=f"wq{e}", align_bytes=64)
-            wsc = sb.tile([P, NQ], U8, name=f"wsc{e}", align_bytes=64)
-            nc.vector.quantize_mx(out=wq[:].bitcast(FP8X4), scales=wsc[:], in_=w[e].rearrange("p q t -> p (q t)"))
             for c in range(2):
                 vc = slice(e * DV + c * (DV // 2), e * DV + (c + 1) * (DV // 2))
                 nc.tensor.matmul_mx(
                     out=acc[c][:],
-                    lhsT=wq[:].bitcast(FP8X4),
-                    lhsT_scale=wsc[:],
+                    lhsT=wq[e][:].bitcast(FP8X4),
+                    lhsT_scale=wsc[e][:],
                     rhs=vg[:, vc].bitcast(FP8X4),
                     rhs_scale=v_plane[V_PLANE:P, vc],
                     start=(e == 0),
                     stop=(e == PAGES - 1),
                 )
 
-        for e in range(PAGES):
-            weigh(e)
-        for e in range(PAGES):
-            product(e)
+        halves = (slice(0, NQ // 2), slice(NQ // 2, NQ))
+        weigh(0, slice(0, NQ))
+        weigh(1, halves[0])
+        quantise(0, slice(0, NQ))
+        product(0)
+        weigh(1, halves[1])
+        for q in halves:
+            quantise(1, q)
+        product(1)
 
         y0 = sb.tile([P, DV // 2], F32, name="y0")
         y1 = sb.tile([P, DV // 2], F32, name="y1")

@@ -27,8 +27,9 @@ DV = 256
 NQ = 128
 VS_ROW = P - 1
 V_PLANE = 4
-VS_SPLIT = 2240
-PIECE = 4096
+VS_SPLIT = 2048
+K_HEAD = 1024
+PIECE = 6144
 FLOPS = 2 * NQ * SLOTS * (D + DV)
 BYTES = (POOL * (D + DV) + NQ * D) * 33 // 32 + POOL * 4 + P * (SLOTS + PAGES * DV) // 8 + NQ * DV * 4
 
@@ -45,9 +46,8 @@ def tile_attend_pkv8q_sigm_cap_kernel(
         offs_t = sb.tile([P, SLOTS // 16], U16, name="offs_t")
         voffs_t = sb.tile([P, PAGES * DV // 16], U16, name="voffs_t")
         kw = sb.tile([P, POOL], I32, name="kw")
-        ks = sb.tile([P, POOL], U8, name="ks")
+        ks = sb.tile([P, POOL], U8, name="ks", tag="key_scales", align_bytes=64)
         vst = sb.tile([P, POOL], F32, name="vst")
-        vw = sb.tile([P, POOL_PAGES * DV], I32, name="vw")
         vsc = sb.tile([P, POOL_PAGES * DV], U8, name="vsc")
         qw = sb.tile([P, NQ], I32, name="qw", align_bytes=64)
         qs = sb.tile([P, NQ], U8, name="qs", align_bytes=64)
@@ -63,37 +63,56 @@ def tile_attend_pkv8q_sigm_cap_kernel(
         ks_words = ks[:].bitcast(I32)
         vs_words = vst[0:VS_ROW, :].bitcast(I32)
         vsc_words = vsc[:].bitcast(I32)
-        nc.gpsimd.memset(warm_in[:], 0.0)
-        fill_odd(vsc_words, 0, 256)
-        nc.gpsimd.memset(vsc_words[:, 256:512], 0)
         fill_odd(ks_words, 0, 512)
         nc.gpsimd.memset(ks_words[:, 512:1024], 0)
+        fill_odd(vsc_words, 0, 256)
+        nc.gpsimd.memset(vsc_words[:, 256:512], 0)
         nc.gpsimd.memset(qs[:].bitcast(I32), 0)
+        nc.gpsimd.memset(warm_in[:], 0.0)
         fill_odd(vs_words, 0, VS_SPLIT)
         nc.gpsimd.memset(vs_words[:, VS_SPLIT:POOL], 0)
+        k_plane = sb.tile([P, SLOTS], U8, name="k_plane", align_bytes=64)
+        v_plane = sb.tile([P, PAGES * DV], U8, name="v_plane", align_bytes=64)
+        nc.gpsimd.memset(k_plane[:].bitcast(I32), 0)
         make_identity(nc, ident[:])
+        nc.gpsimd.memset(v_plane[:].bitcast(I32), 0)
 
-        nc.scalar.dma_start(vst[VS_ROW : VS_ROW + 1, :], vs[0:1, :])
-        nc.scalar.dma_start(
-            kw[:], k_words[0].rearrange("p n t -> p (n t)").bitcast(I32), max_dma_last_dim=PIECE
-        )
+        def q_scale_rows(r):
+            nc.sync.dma_start(qs[r:P:32, :].bitcast(I32), q_scales[0, 0, r:16:4, :].bitcast(I32))
+
+        k_src = k_words[0].rearrange("p n t -> p (n t)").bitcast(I32)
+        nc.scalar.dma_start(qw[:], q_words[0, 0].rearrange("p n t -> p (n t)").bitcast(I32))
+        nc.scalar.dma_start(kw[:, 0:K_HEAD], k_src[:, 0:K_HEAD])
         nc.scalar.activation(warm[:], warm_in[:], ACT.Tanh)
         nc.sync.dma_start(offs_t[:], offs)
+        nc.sync.dma_start(voffs_t[:], voffs)
+        nc.sync.dma_start(ks[0:P:8, :].bitcast(I32), k_scales[0].bitcast(I32))
+        nc.sync.dma_start(vst[VS_ROW : VS_ROW + 1, :], vs[0:1, :])
         nc.sync.dma_start(
             vsc[V_PLANE:P:8, :].bitcast(I32).rearrange("p (u c) -> p u c", u=POOL_PAGES),
             v_scales.bitcast(I32).rearrange("u f c -> f u c"),
         )
-        for r in range(4):
-            nc.sync.dma_start(ks[r:P:32, :].bitcast(I32), k_scales[0, r:16:4, :].bitcast(I32))
-        nc.sync.dma_start(voffs_t[:], voffs)
-        nc.sync.dma_start(qw[:], q_words[0, 0].rearrange("p n t -> p (n t)").bitcast(I32))
-        for r in range(4):
-            nc.sync.dma_start(qs[r:P:32, :].bitcast(I32), q_scales[0, 0, r:16:4, :].bitcast(I32))
+        q_scale_rows(0)
+        q_scale_rows(1)
+        nc.sync.dma_start(kw[:, K_HEAD:POOL], k_src[:, K_HEAD:POOL], max_dma_last_dim=PIECE)
+        q_scale_rows(2)
+        q_scale_rows(3)
 
         ksg = sb.tile([P, SLOTS], U8, name="ksg", align_bytes=64)
         nc.vector.tensor_copy(ksg[:], ks[:].indirect(offs_t[:]))
+        for r in range(4):
+            nc.sync.dma_start(k_plane[r:P:32, :].bitcast(I32), ksg[8 * r : P : 32, :].bitcast(I32))
+        vw = sb.tile([P, POOL_PAGES * DV], I32, name="vw", tag="key_scales", align_bytes=64)
+        nc.sync.dma_start(
+            vw[:].rearrange("p (u e) -> p u e", u=POOL_PAGES),
+            v_words.rearrange("u p e t -> p u (e t)").bitcast(I32),
+        )
         vscg = sb.tile([P, PAGES * DV], U8, name="vscg", align_bytes=64)
         nc.vector.tensor_copy(vscg[:], vsc[:].indirect(voffs_t[:]))
+        for r in range(4):
+            nc.sync.dma_start(
+                v_plane[V_PLANE + r : P : 32, :].bitcast(I32), vscg[V_PLANE + 8 * r : P : 32, :].bitcast(I32)
+            )
 
         page_cols = PAGE // 16
         chunk_cols = CHUNK // 16
@@ -109,22 +128,11 @@ def tile_attend_pkv8q_sigm_cap_kernel(
 
         gather_vs(0)
         gather_vs(1)
-        nc.scalar.dma_start(
-            vw[:].rearrange("p (u e) -> p u e", u=POOL_PAGES),
-            v_words.rearrange("u p e t -> p u (e t)").bitcast(I32),
-        )
         for e in range(PAGES):
             turned = ps.tile([P, PACK, P], F32, name=f"turned{e}", tag=f"bank{e}")
             for t in range(PACK):
                 nc.tensor.transpose(turned[:, t, :], vsg[:, e * PAGE + t : (e + 1) * PAGE : PACK], ident[:])
             nc.scalar.activation(vs_half[e][:], turned[:, :, VS_ROW], ACT.Copy, scale=0.5)
-
-        v_plane = sb.tile([P, PAGES * DV], U8, name="v_plane", align_bytes=64)
-        nc.gpsimd.memset(v_plane[:].bitcast(I32), 0)
-        for r in range(4):
-            nc.sync.dma_start(
-                v_plane[V_PLANE + r : P : 32, :].bitcast(I32), vscg[V_PLANE + 8 * r : P : 32, :].bitcast(I32)
-            )
 
         banks = []
         for c in range(CHUNKS):
@@ -139,7 +147,7 @@ def tile_attend_pkv8q_sigm_cap_kernel(
                 lhsT=qw[:].bitcast(FP8X4),
                 lhsT_scale=qs[:],
                 rhs=kg[:].bitcast(FP8X4),
-                rhs_scale=ksg[:, cols],
+                rhs_scale=k_plane[:, cols],
                 start=True,
                 stop=True,
             )
@@ -163,7 +171,8 @@ def tile_attend_pkv8q_sigm_cap_kernel(
                 nc.tensor.transpose(flipped[e][:, t, :], half_cap[e][:, t, :], ident[:])
 
         th = [sb.tile([P, NQ, PACK], F32, name=f"th{e}") for e in range(PAGES)]
-        w = [sb.tile([P, NQ, PACK], BF16, name=f"w{e}", align_bytes=64) for e in range(PAGES)]
+        w_all = sb.tile([P, PAGES, NQ, PACK], BF16, name="w_all", tag="key_scales", align_bytes=64)
+        w = [w_all[:, e] for e in range(PAGES)]
         wq = [sb.tile([P, NQ], U32, name=f"wq{e}", align_bytes=64) for e in range(PAGES)]
         wsc = [sb.tile([P, NQ], U8, name=f"wsc{e}", align_bytes=64) for e in range(PAGES)]
         acc = [ps.tile([P, DV // 2], F32, name=f"acc{c}", tag=f"bank{c}") for c in range(2)]

@@ -27,6 +27,7 @@ DV = 256
 NQ = 128
 VS_ROW = P - 1
 V_PLANE = 4
+SPREAD = 28
 VS_SPLIT = 2048
 K_HEAD = 1024
 PIECE = 6144
@@ -86,10 +87,10 @@ def tile_attend_pkv8q_sigm_cap_kernel(
         nc.scalar.activation(warm[:], warm_in[:], ACT.Tanh)
         nc.sync.dma_start(offs_t[:], offs)
         nc.sync.dma_start(voffs_t[:], voffs)
-        nc.sync.dma_start(ks[0:P:8, :].bitcast(I32), k_scales[0].bitcast(I32))
+        nc.sync.dma_start(ks[SPREAD : SPREAD + 64 : 4, :].bitcast(I32), k_scales[0].bitcast(I32))
         nc.sync.dma_start(vst[VS_ROW : VS_ROW + 1, :], vs[0:1, :])
         nc.sync.dma_start(
-            vsc[V_PLANE:P:8, :].bitcast(I32).rearrange("p (u c) -> p u c", u=POOL_PAGES),
+            vsc[SPREAD : SPREAD + 64 : 4, :].bitcast(I32).rearrange("p (u c) -> p u c", u=POOL_PAGES),
             v_scales.bitcast(I32).rearrange("u f c -> f u c"),
         )
         q_scale_rows(0)
@@ -101,7 +102,9 @@ def tile_attend_pkv8q_sigm_cap_kernel(
         ksg = sb.tile([P, SLOTS], U8, name="ksg", align_bytes=64)
         nc.vector.tensor_copy(ksg[:], ks[:].indirect(offs_t[:]))
         for r in range(4):
-            nc.sync.dma_start(k_plane[r:P:32, :].bitcast(I32), ksg[8 * r : P : 32, :].bitcast(I32))
+            nc.sync.dma_start(
+                k_plane[r:P:32, :].bitcast(I32), ksg[SPREAD + 4 * r : SPREAD + 64 : 16, :].bitcast(I32)
+            )
         vw = sb.tile([P, POOL_PAGES * DV], I32, name="vw", tag="key_scales", align_bytes=64)
         nc.sync.dma_start(
             vw[:].rearrange("p (u e) -> p u e", u=POOL_PAGES),
@@ -111,7 +114,8 @@ def tile_attend_pkv8q_sigm_cap_kernel(
         nc.vector.tensor_copy(vscg[:], vsc[:].indirect(voffs_t[:]))
         for r in range(4):
             nc.sync.dma_start(
-                v_plane[V_PLANE + r : P : 32, :].bitcast(I32), vscg[V_PLANE + 8 * r : P : 32, :].bitcast(I32)
+                v_plane[V_PLANE + r : P : 32, :].bitcast(I32),
+                vscg[SPREAD + 4 * r : SPREAD + 64 : 16, :].bitcast(I32),
             )
 
         page_cols = PAGE // 16

@@ -27,10 +27,9 @@ DV = 256
 NQ = 128
 VS_ROW = P - 1
 V_PLANE = 4
-SPREAD = 28
+SPREAD = 32
 VS_SPLIT = 2048
 K_HEAD = 1024
-PIECE = 6144
 FLOPS = 2 * NQ * SLOTS * (D + DV)
 BYTES = (POOL * (D + DV) + NQ * D) * 33 // 32 + POOL * 4 + P * (SLOTS + PAGES * DV) // 8 + NQ * DV * 4
 
@@ -95,7 +94,7 @@ def tile_attend_pkv8q_sigm_cap_kernel(
         )
         q_scale_rows(0)
         q_scale_rows(1)
-        nc.sync.dma_start(kw[:, K_HEAD:POOL], k_src[:, K_HEAD:POOL], max_dma_last_dim=PIECE)
+        nc.sync.dma_start(kw[:, K_HEAD:POOL], k_src[:, K_HEAD:POOL])
         q_scale_rows(2)
         q_scale_rows(3)
 

@@ -14,6 +14,7 @@ ACT = mybir.ActivationFunctionType
 ALU = mybir.AluOpType
 
 P = 128
+QUADRANT = 32
 PACK = 4
 PAGE = 512
 PAGES = 2
@@ -25,13 +26,20 @@ POOL_PAGES = POOL // PAGE
 D = 512
 DV = 256
 NQ = 128
+HALF = NQ // 2
 VS_ROW = P - 1
 V_PLANE = 4
 SPREAD = 32
-VS_SPLIT = 2048
-K_HEAD = 1024
+VS_SPLIT = 1792
+K_HEAD = 512
 FLOPS = 2 * NQ * SLOTS * (D + DV)
 BYTES = (POOL * (D + DV) + NQ * D) * 33 // 32 + POOL * 4 + P * (SLOTS + PAGES * DV) // 8 + NQ * DV * 4
+
+KEYS_AT = 0
+SCALES_AT = KEYS_AT + 4 * POOL
+VALUES_AT = SCALES_AT + POOL
+GATHERED_AT = VALUES_AT + 4 * POOL_PAGES * DV
+PROBS_AT = GATHERED_AT + 4 * SLOTS
 
 
 def tile_attend_pkv8q_sigm_cap_kernel(
@@ -45,12 +53,13 @@ def tile_attend_pkv8q_sigm_cap_kernel(
 
         offs_t = sb.tile([P, SLOTS // 16], U16, name="offs_t")
         voffs_t = sb.tile([P, PAGES * DV // 16], U16, name="voffs_t")
-        kw = sb.tile([P, POOL], I32, name="kw")
-        ks = sb.tile([P, POOL], U8, name="ks", tag="key_scales", align_bytes=64)
+        kw = shared.tile([P, POOL], I32, name="kw", offset=KEYS_AT, align_bytes=64)
+        ks = shared.tile([P, POOL], U8, name="ks", offset=SCALES_AT, align_bytes=64)
         vst = sb.tile([P, POOL], F32, name="vst")
-        vsc = sb.tile([P, POOL_PAGES * DV], U8, name="vsc")
         qw = sb.tile([P, NQ], I32, name="qw", align_bytes=64)
-        qs = sb.tile([P, NQ], U8, name="qs", align_bytes=64)
+        q_rows = shared.tile([P, 4, NQ // 4], I32, name="q_rows", offset=VALUES_AT, align_bytes=64)
+        k_plane = sb.tile([P, SLOTS], U8, name="k_plane", align_bytes=64)
+        v_plane = sb.tile([P, PAGES * DV], U8, name="v_plane", align_bytes=64)
         ident = sb.tile([P, P], F32, name="ident")
         warm = sb.tile([P, 1], F32, name="warm")
         warm_in = sb.tile([P, 1], F32, name="warm_in")
@@ -62,100 +71,95 @@ def tile_attend_pkv8q_sigm_cap_kernel(
 
         ks_words = ks[:].bitcast(I32)
         vs_words = vst[0:VS_ROW, :].bitcast(I32)
-        vsc_words = vsc[:].bitcast(I32)
         fill_odd(ks_words, 0, 512)
         nc.gpsimd.memset(ks_words[:, 512:1024], 0)
-        fill_odd(vsc_words, 0, 256)
-        nc.gpsimd.memset(vsc_words[:, 256:512], 0)
-        nc.gpsimd.memset(qs[:].bitcast(I32), 0)
         nc.gpsimd.memset(warm_in[:], 0.0)
         fill_odd(vs_words, 0, VS_SPLIT)
         nc.gpsimd.memset(vs_words[:, VS_SPLIT:POOL], 0)
-        k_plane = sb.tile([P, SLOTS], U8, name="k_plane", align_bytes=64)
-        v_plane = sb.tile([P, PAGES * DV], U8, name="v_plane", align_bytes=64)
         nc.gpsimd.memset(k_plane[:].bitcast(I32), 0)
         make_identity(nc, ident[:])
         nc.gpsimd.memset(v_plane[:].bitcast(I32), 0)
 
-        def q_scale_rows(r):
-            nc.sync.dma_start(qs[r:P:32, :].bitcast(I32), q_scales[0, 0, r:16:4, :].bitcast(I32))
-
         k_src = k_words[0].rearrange("p n t -> p (n t)").bitcast(I32)
-        nc.scalar.dma_start(qw[:], q_words[0, 0].rearrange("p n t -> p (n t)").bitcast(I32))
         nc.scalar.dma_start(kw[:, 0:K_HEAD], k_src[:, 0:K_HEAD])
-        nc.scalar.activation(warm[:], warm_in[:], ACT.Tanh)
+        nc.scalar.activation(warm[:], warm_in[:], ACT.Sigmoid)
         nc.sync.dma_start(offs_t[:], offs)
+        nc.sync.dma_start(q_rows[0:4], q_scales[0, 0].bitcast(I32).rearrange("(g r) c -> r g c", r=4))
         nc.sync.dma_start(voffs_t[:], voffs)
         nc.sync.dma_start(ks[SPREAD : SPREAD + 64 : 4, :].bitcast(I32), k_scales[0].bitcast(I32))
         nc.sync.dma_start(vst[VS_ROW : VS_ROW + 1, :], vs[0:1, :])
+        nc.sync.dma_start(kw[:, K_HEAD:POOL], k_src[:, K_HEAD:POOL])
+        nc.sync.dma_start(qw[:], q_words[0, 0].rearrange("p n t -> p (n t)").bitcast(I32))
+
+        ksg = sb.tile([P, SLOTS], U8, name="ksg", align_bytes=64)
+        nc.vector.tensor_copy(ksg[:], ks[:].indirect(offs_t[:]))
+        vsc = shared.tile([P, POOL_PAGES * DV], U8, name="vsc", offset=SCALES_AT, align_bytes=64)
+        nc.vector.memset(vsc[:].bitcast(I32), 0)
+        q_plane = shared.tile([P, NQ], U8, name="q_plane", offset=SCALES_AT + POOL_PAGES * DV, align_bytes=64)
+        nc.vector.memset(q_plane[:].bitcast(I32), 0)
+        for g in range(4):
+            nc.vector.tensor_copy(q_plane[QUADRANT * g : QUADRANT * g + 4, :].bitcast(I32), q_rows[0:4, g, :])
+        for r in range(4):
+            nc.sync.dma_start(
+                k_plane[r:P:QUADRANT, :].bitcast(I32), ksg[SPREAD + 4 * r : SPREAD + 64 : 16, :].bitcast(I32)
+            )
         nc.sync.dma_start(
             vsc[SPREAD : SPREAD + 64 : 4, :].bitcast(I32).rearrange("p (u c) -> p u c", u=POOL_PAGES),
             v_scales.bitcast(I32).rearrange("u f c -> f u c"),
         )
-        q_scale_rows(0)
-        q_scale_rows(1)
-        nc.sync.dma_start(kw[:, K_HEAD:POOL], k_src[:, K_HEAD:POOL])
-        q_scale_rows(2)
-        q_scale_rows(3)
-
-        ksg = sb.tile([P, SLOTS], U8, name="ksg", align_bytes=64)
-        nc.vector.tensor_copy(ksg[:], ks[:].indirect(offs_t[:]))
-        for r in range(4):
-            nc.sync.dma_start(
-                k_plane[r:P:32, :].bitcast(I32), ksg[SPREAD + 4 * r : SPREAD + 64 : 16, :].bitcast(I32)
-            )
-        vw = sb.tile([P, POOL_PAGES * DV], I32, name="vw", tag="key_scales", align_bytes=64)
+        vw = shared.tile([P, POOL_PAGES * DV], I32, name="vw", offset=VALUES_AT, align_bytes=64)
         nc.sync.dma_start(
             vw[:].rearrange("p (u e) -> p u e", u=POOL_PAGES),
             v_words.rearrange("u p e t -> p u (e t)").bitcast(I32),
         )
-        vscg = sb.tile([P, PAGES * DV], U8, name="vscg", align_bytes=64)
-        nc.vector.tensor_copy(vscg[:], vsc[:].indirect(voffs_t[:]))
-        for r in range(4):
-            nc.sync.dma_start(
-                v_plane[V_PLANE + r : P : 32, :].bitcast(I32),
-                vscg[SPREAD + 4 * r : SPREAD + 64 : 16, :].bitcast(I32),
-            )
 
         page_cols = PAGE // 16
         chunk_cols = CHUNK // 16
-        vsg = shared.tile([P, SLOTS], F32, name="vsg", offset=0, align_bytes=64)
-        vs_half = [sb.tile([P, PACK], F32, name=f"vs_half{e}", align_bytes=64) for e in range(PAGES)]
-
-        def gather_vs(e):
+        vsg = shared.tile([P, SLOTS], F32, name="vsg", offset=GATHERED_AT, align_bytes=64)
+        for e in range(PAGES):
             nc.scalar.activation(
                 vsg[:, e * PAGE : (e + 1) * PAGE],
                 vst[:].indirect(offs_t[:, e * page_cols : (e + 1) * page_cols]),
                 ACT.Copy,
             )
-
-        gather_vs(0)
-        gather_vs(1)
+        turned = [ps.tile([P, PACK, P], F32, name=f"turned{e}") for e in range(PAGES)]
         for e in range(PAGES):
-            turned = ps.tile([P, PACK, P], F32, name=f"turned{e}", tag=f"bank{e}")
             for t in range(PACK):
-                nc.tensor.transpose(turned[:, t, :], vsg[:, e * PAGE + t : (e + 1) * PAGE : PACK], ident[:])
-            nc.scalar.activation(vs_half[e][:], turned[:, :, VS_ROW], ACT.Copy, scale=0.5)
+                nc.tensor.transpose(turned[e][:, t, :], vsg[:, e * PAGE + t : (e + 1) * PAGE : PACK], ident[:])
+
+        def vs_by_query(e):
+            return turned[e][:, :, VS_ROW].unsqueeze(1).to_broadcast([P, HALF, PACK])
+
+        vs_wide = sb.tile([P, HALF, PACK], F32, name="vs_wide")
+        nc.scalar.activation(vs_wide[:], vs_by_query(0), ACT.Copy)
 
         banks = []
         for c in range(CHUNKS):
             cols = slice(c * CHUNK, (c + 1) * CHUNK)
-            kg = shared.tile([P, CHUNK], U32, name=f"kg{c}", offset=4 * CHUNK * c, align_bytes=64)
+            kg = sb.tile([P, CHUNK], U32, name=f"kg{c}", align_bytes=64)
             nc.vector.tensor_copy(
                 kg[:], kw[:].bitcast(U32).indirect(offs_t[:, c * chunk_cols : (c + 1) * chunk_cols])
             )
-            bank = ps.tile([P, CHUNK], F32, name=f"score{c}")
+            bank = ps.tile([P, CHUNK], F32, name=f"score{c}", tag=f"bank{c}")
             nc.tensor.matmul_mx(
                 out=bank[:],
                 lhsT=qw[:].bitcast(FP8X4),
-                lhsT_scale=qs[:],
+                lhsT_scale=q_plane[:],
                 rhs=kg[:].bitcast(FP8X4),
                 rhs_scale=k_plane[:, cols],
                 start=True,
                 stop=True,
             )
             banks.append(bank)
-        vg = shared.tile([P, PAGES * DV], U32, name="vg", offset=0, align_bytes=64)
+
+        vscg = shared.tile([P, PAGES * DV], U8, name="vscg", offset=KEYS_AT, align_bytes=64)
+        nc.vector.tensor_copy(vscg[:], vsc[:].indirect(voffs_t[:]))
+        for r in range(4):
+            nc.sync.dma_start(
+                v_plane[V_PLANE + r : P : QUADRANT, :].bitcast(I32),
+                vscg[SPREAD + 4 * r : SPREAD + 64 : 16, :].bitcast(I32),
+            )
+        vg = shared.tile([P, PAGES * DV], U32, name="vg", offset=KEYS_AT + 1024, align_bytes=64)
         nc.vector.tensor_copy(vg[:], vw[:].bitcast(U32).indirect(voffs_t[:]))
 
         rows = CHUNK // PACK
@@ -173,27 +177,51 @@ def tile_attend_pkv8q_sigm_cap_kernel(
             for t in range(PACK):
                 nc.tensor.transpose(flipped[e][:, t, :], half_cap[e][:, t, :], ident[:])
 
-        th = [sb.tile([P, NQ, PACK], F32, name=f"th{e}") for e in range(PAGES)]
-        w_all = sb.tile([P, PAGES, NQ, PACK], BF16, name="w_all", tag="key_scales", align_bytes=64)
-        w = [w_all[:, e] for e in range(PAGES)]
-        wq = [sb.tile([P, NQ], U32, name=f"wq{e}", align_bytes=64) for e in range(PAGES)]
-        wsc = [sb.tile([P, NQ], U8, name=f"wsc{e}", align_bytes=64) for e in range(PAGES)]
+        pieces = [(e, h) for e in range(PAGES) for h in range(2)]
+        prob = {}
+        w = {}
+        for i, (e, h) in enumerate(pieces):
+            prob[e, h] = shared.tile(
+                [P, HALF, PACK], F32, name=f"prob{e}{h}", offset=PROBS_AT + 1024 * i, align_bytes=64
+            )
+        w[0, 0] = sb.tile([P, HALF, PACK], BF16, name="w00", align_bytes=64)
+        for i, (e, h) in enumerate(pieces[1:]):
+            w[e, h] = shared.tile(
+                [P, HALF, PACK], BF16, name=f"w{e}{h}", offset=VALUES_AT + 2048 + 512 * i, align_bytes=64
+            )
         acc = [ps.tile([P, DV // 2], F32, name=f"acc{c}", tag=f"bank{c}") for c in range(2)]
 
-        def weigh(e, q):
-            nc.scalar.activation(th[e][:, q, :], flipped[e][:, :, q].rearrange("p t q -> p q t"), ACT.Tanh)
-            nc.vector.scalar_tensor_tensor(
-                out=w[e][:, q, :],
-                in0=th[e][:, q, :],
-                scalar=1.0,
-                in1=vs_half[e][:].unsqueeze(1).to_broadcast([P, q.stop - q.start, PACK]),
-                op0=ALU.add,
-                op1=ALU.mult,
+        def query_cols(h):
+            return slice(h * HALF, (h + 1) * HALF)
+
+        for e, h in pieces:
+            nc.scalar.activation(
+                prob[e, h][:], flipped[e][:, :, query_cols(h)].rearrange("p t q -> p q t"), ACT.Sigmoid, scale=2.0
             )
 
-        def quantise(e, q):
+        def weigh(e, h):
+            nc.vector.tensor_tensor(w[e, h][:], prob[e, h][:], vs_by_query(e), ALU.mult)
+
+        nc.gpsimd.tensor_tensor(
+            w[0, 0][:].rearrange("p q t -> p (q t)"),
+            prob[0, 0][:].rearrange("p q t -> p (q t)"),
+            vs_wide[:].rearrange("p q t -> p (q t)"),
+            ALU.mult,
+        )
+        weigh(0, 1)
+        weigh(1, 0)
+
+        wq = [
+            shared.tile([P, NQ], U32, name="wq0", offset=PROBS_AT + 1024, align_bytes=64),
+            sb.tile([P, NQ], U32, name="wq1", align_bytes=64),
+        ]
+        wsc = [sb.tile([P, NQ], U8, name=f"wsc{e}", align_bytes=64) for e in range(PAGES)]
+
+        def quantise(e, h):
             nc.vector.quantize_mx(
-                out=wq[e][:, q].bitcast(FP8X4), scales=wsc[e][:, q], in_=w[e][:, q, :].rearrange("p q t -> p (q t)")
+                out=wq[e][:, query_cols(h)].bitcast(FP8X4),
+                scales=wsc[e][:, query_cols(h)],
+                in_=w[e, h][:].rearrange("p q t -> p (q t)"),
             )
 
         def product(e):
@@ -209,14 +237,12 @@ def tile_attend_pkv8q_sigm_cap_kernel(
                     stop=(e == PAGES - 1),
                 )
 
-        halves = (slice(0, NQ // 2), slice(NQ // 2, NQ))
-        weigh(0, slice(0, NQ))
-        weigh(1, halves[0])
-        quantise(0, slice(0, NQ))
+        quantise(0, 1)
+        quantise(0, 0)
         product(0)
-        weigh(1, halves[1])
-        for q in halves:
-            quantise(1, q)
+        weigh(1, 1)
+        quantise(1, 0)
+        quantise(1, 1)
         product(1)
 
         y0 = sb.tile([P, DV // 2], F32, name="y0")

@@ -30,7 +30,8 @@ HALF = NQ // 2
 VS_ROW = P - 1
 V_PLANE = 4
 SPREAD = 32
-VS_SPLIT = 1792
+KS_SPLIT = 416
+VS_SPLIT = 1760
 K_HEAD = 512
 FLOPS = 2 * NQ * SLOTS * (D + DV)
 BYTES = (POOL * (D + DV) + NQ * D) * 33 // 32 + POOL * 4 + P * (SLOTS + PAGES * DV) // 8 + NQ * DV * 4
@@ -71,8 +72,8 @@ def tile_attend_pkv8q_sigm_cap_kernel(
 
         ks_words = ks[:].bitcast(I32)
         vs_words = vst[0:VS_ROW, :].bitcast(I32)
-        fill_odd(ks_words, 0, 512)
-        nc.gpsimd.memset(ks_words[:, 512:1024], 0)
+        fill_odd(ks_words, 0, KS_SPLIT)
+        nc.gpsimd.memset(ks_words[:, KS_SPLIT : POOL // 4], 0)
         nc.gpsimd.memset(warm_in[:], 0.0)
         fill_odd(vs_words, 0, VS_SPLIT)
         nc.gpsimd.memset(vs_words[:, VS_SPLIT:POOL], 0)
@@ -93,10 +94,10 @@ def tile_attend_pkv8q_sigm_cap_kernel(
 
         ksg = sb.tile([P, SLOTS], U8, name="ksg", align_bytes=64)
         nc.vector.tensor_copy(ksg[:], ks[:].indirect(offs_t[:]))
-        vsc = shared.tile([P, POOL_PAGES * DV], U8, name="vsc", offset=SCALES_AT, align_bytes=64)
-        nc.vector.memset(vsc[:].bitcast(I32), 0)
         q_plane = shared.tile([P, NQ], U8, name="q_plane", offset=SCALES_AT + POOL_PAGES * DV, align_bytes=64)
         nc.vector.memset(q_plane[:].bitcast(I32), 0)
+        vsc = shared.tile([P, POOL_PAGES * DV], U8, name="vsc", offset=SCALES_AT, align_bytes=64)
+        nc.vector.memset(vsc[:].bitcast(I32), 0)
         for g in range(4):
             nc.vector.tensor_copy(q_plane[QUADRANT * g : QUADRANT * g + 4, :].bitcast(I32), q_rows[0:4, g, :])
         for r in range(4):

from contextlib import ExitStack

import concourse.mybir as mybir
from concourse.masks import make_identity

F32 = mybir.dt.float32
BF16 = mybir.dt.bfloat16
I32 = mybir.dt.int32
U32 = mybir.dt.uint32
U16 = mybir.dt.uint16
U8 = mybir.dt.uint8
FP8X4 = mybir.dt.float8_e4m3fn_x4
ACT = mybir.ActivationFunctionType
ALU = mybir.AluOpType

P = 128
QUADRANT = 32
PACK = 4
PAGE = 512
PAGES = 2
SLOTS = PAGE * PAGES
CHUNK = 256
CHUNKS = SLOTS // CHUNK
POOL = 4096
POOL_PAGES = POOL // PAGE
D = 512
DV = 256
NQ = 128
HALF = NQ // 2
VS_ROW = P - 1
V_PLANE = 4
SPREAD = 32
KS_SPLIT = 416
VS_SPLIT = 1760
K_HEAD = 512
FLOPS = 2 * NQ * SLOTS * (D + DV)
BYTES = (POOL * (D + DV) + NQ * D) * 33 // 32 + POOL * 4 + P * (SLOTS + PAGES * DV) // 8 + NQ * DV * 4

KEYS_AT = 0
SCALES_AT = KEYS_AT + 4 * POOL
VALUES_AT = SCALES_AT + POOL
GATHERED_AT = VALUES_AT + 4 * POOL_PAGES * DV
PROBS_AT = GATHERED_AT + 4 * SLOTS


def tile_attend_pkv8q_sigm_cap_kernel(
    tc, q_words, q_scales, k_words, k_scales, v_words, v_scales, vs, offs, voffs, out
):
    nc = tc.nc
    with ExitStack() as ctx:
        sb = ctx.enter_context(tc.tile_pool(name="sb", bufs=1))
        shared = ctx.enter_context(tc.tile_pool(name="shared", bufs=1))
        ps = ctx.enter_context(tc.psum_pool(name="ps", bufs=1))

        offs_t = sb.tile([P, SLOTS // 16], U16, name="offs_t")
        voffs_t = sb.tile([P, PAGES * DV // 16], U16, name="voffs_t")
        kw = shared.tile([P, POOL], I32, name="kw", offset=KEYS_AT, align_bytes=64)
        ks = shared.tile([P, POOL], U8, name="ks", offset=SCALES_AT, align_bytes=64)
        vst = sb.tile([P, POOL], F32, name="vst")
        qw = sb.tile([P, NQ], I32, name="qw", align_bytes=64)
        q_rows = shared.tile([P, 4, NQ // 4], I32, name="q_rows", offset=VALUES_AT, align_bytes=64)
        k_plane = sb.tile([P, SLOTS], U8, name="k_plane", align_bytes=64)
        v_plane = sb.tile([P, PAGES * DV], U8, name="v_plane", align_bytes=64)
        ident = sb.tile([P, P], F32, name="ident")
        warm = sb.tile([P, 1], F32, name="warm")
        warm_in = sb.tile([P, 1], F32, name="warm_in")

        def fill_odd(view, a, b):
            m = a + (b - a) // 2 - 1 + ((b - a) // 2) % 2
            nc.vector.memset(view[:, a:m], 0)
            nc.vector.memset(view[:, m:b], 0)

        ks_words = ks[:].bitcast(I32)
        vs_words = vst[0:VS_ROW, :].bitcast(I32)
        fill_odd(ks_words, 0, KS_SPLIT)
        nc.gpsimd.memset(ks_words[:, KS_SPLIT : POOL // 4], 0)
        nc.gpsimd.memset(warm_in[:], 0.0)
        fill_odd(vs_words, 0, VS_SPLIT)
        nc.gpsimd.memset(vs_words[:, VS_SPLIT:POOL], 0)
        nc.gpsimd.memset(k_plane[:].bitcast(I32), 0)
        make_identity(nc, ident[:])
        nc.gpsimd.memset(v_plane[:].bitcast(I32), 0)

        k_src = k_words[0].rearrange("p n t -> p (n t)").bitcast(I32)
        nc.scalar.dma_start(kw[:, 0:K_HEAD], k_src[:, 0:K_HEAD])
        nc.scalar.activation(warm[:], warm_in[:], ACT.Sigmoid)
        nc.sync.dma_start(offs_t[:], offs)
        nc.sync.dma_start(q_rows[0:4], q_scales[0, 0].bitcast(I32).rearrange("(g r) c -> r g c", r=4))
        nc.sync.dma_start(voffs_t[:], voffs)
        nc.sync.dma_start(ks[SPREAD : SPREAD + 64 : 4, :].bitcast(I32), k_scales[0].bitcast(I32))
        nc.sync.dma_start(vst[VS_ROW : VS_ROW + 1, :], vs[0:1, :])
        nc.sync.dma_start(kw[:, K_HEAD:POOL], k_src[:, K_HEAD:POOL])
        nc.sync.dma_start(qw[:], q_words[0, 0].rearrange("p n t -> p (n t)").bitcast(I32))

        ksg = sb.tile([P, SLOTS], U8, name="ksg", align_bytes=64)
        nc.vector.tensor_copy(ksg[:], ks[:].indirect(offs_t[:]))
        q_plane = shared.tile([P, NQ], U8, name="q_plane", offset=SCALES_AT + POOL_PAGES * DV, align_bytes=64)
        nc.vector.memset(q_plane[:].bitcast(I32), 0)
        vsc = shared.tile([P, POOL_PAGES * DV], U8, name="vsc", offset=SCALES_AT, align_bytes=64)
        nc.vector.memset(vsc[:].bitcast(I32), 0)
        for g in range(4):
            nc.vector.tensor_copy(q_plane[QUADRANT * g : QUADRANT * g + 4, :].bitcast(I32), q_rows[0:4, g, :])
        for r in range(4):
            nc.sync.dma_start(
                k_plane[r:P:QUADRANT, :].bitcast(I32), ksg[SPREAD + 4 * r : SPREAD + 64 : 16, :].bitcast(I32)
            )
        nc.sync.dma_start(
            vsc[SPREAD : SPREAD + 64 : 4, :].bitcast(I32).rearrange("p (u c) -> p u c", u=POOL_PAGES),
            v_scales.bitcast(I32).rearrange("u f c -> f u c"),
        )
        vw = shared.tile([P, POOL_PAGES * DV], I32, name="vw", offset=VALUES_AT, align_bytes=64)
        nc.sync.dma_start(
            vw[:].rearrange("p (u e) -> p u e", u=POOL_PAGES),
            v_words.rearrange("u p e t -> p u (e t)").bitcast(I32),
        )

        page_cols = PAGE // 16
        chunk_cols = CHUNK // 16
        vsg = shared.tile([P, SLOTS], F32, name="vsg", offset=GATHERED_AT, align_bytes=64)
        for e in range(PAGES):
            nc.scalar.activation(
                vsg[:, e * PAGE : (e + 1) * PAGE],
                vst[:].indirect(offs_t[:, e * page_cols : (e + 1) * page_cols]),
                ACT.Copy,
            )
        turned = [ps.tile([P, PACK, P], F32, name=f"turned{e}") for e in range(PAGES)]
        for e in range(PAGES):
            for t in range(PACK):
                nc.tensor.transpose(turned[e][:, t, :], vsg[:, e * PAGE + t : (e + 1) * PAGE : PACK], ident[:])

        def vs_by_query(e):
            return turned[e][:, :, VS_ROW].unsqueeze(1).to_broadcast([P, HALF, PACK])

        vs_wide = sb.tile([P, HALF, PACK], F32, name="vs_wide")
        nc.scalar.activation(vs_wide[:], vs_by_query(0), ACT.Copy)

        banks = []
        for c in range(CHUNKS):
            cols = slice(c * CHUNK, (c + 1) * CHUNK)
            kg = sb.tile([P, CHUNK], U32, name=f"kg{c}", align_bytes=64)
            nc.vector.tensor_copy(
                kg[:], kw[:].bitcast(U32).indirect(offs_t[:, c * chunk_cols : (c + 1) * chunk_cols])
            )
            bank = ps.tile([P, CHUNK], F32, name=f"score{c}", tag=f"bank{c}")
            nc.tensor.matmul_mx(
                out=bank[:],
                lhsT=qw[:].bitcast(FP8X4),
                lhsT_scale=q_plane[:],
                rhs=kg[:].bitcast(FP8X4),
                rhs_scale=k_plane[:, cols],
                start=True,
                stop=True,
            )
            banks.append(bank)

        vscg = shared.tile([P, PAGES * DV], U8, name="vscg", offset=KEYS_AT, align_bytes=64)
        nc.vector.tensor_copy(vscg[:], vsc[:].indirect(voffs_t[:]))
        for r in range(4):
            nc.sync.dma_start(
                v_plane[V_PLANE + r : P : QUADRANT, :].bitcast(I32),
                vscg[SPREAD + 4 * r : SPREAD + 64 : 16, :].bitcast(I32),
            )
        vg = shared.tile([P, PAGES * DV], U32, name="vg", offset=KEYS_AT + 1024, align_bytes=64)
        nc.vector.tensor_copy(vg[:], vw[:].bitcast(U32).indirect(voffs_t[:]))

        rows = CHUNK // PACK
        half_cap = [sb.tile([P, PACK, P], F32, name=f"half_cap{e}") for e in range(PAGES)]
        flipped = [ps.tile([P, PACK, NQ], F32, name=f"flipped{e}") for e in range(PAGES)]
        for c in range(CHUNKS):
            e, h = divmod(c, 2)
            nc.scalar.activation(
                half_cap[e][:, :, h * rows : (h + 1) * rows],
                banks[c][:].rearrange("q (p t) -> q t p", t=PACK),
                ACT.Tanh,
                scale=0.5,
            )
        for e in range(PAGES):
            for t in range(PACK):
                nc.tensor.transpose(flipped[e][:, t, :], half_cap[e][:, t, :], ident[:])

        pieces = [(e, h) for e in range(PAGES) for h in range(2)]
        prob = {}
        w = {}
        for i, (e, h) in enumerate(pieces):
            prob[e, h] = shared.tile(
                [P, HALF, PACK], F32, name=f"prob{e}{h}", offset=PROBS_AT + 1024 * i, align_bytes=64
            )
        w[0, 0] = sb.tile([P, HALF, PACK], BF16, name="w00", align_bytes=64)
        for i, (e, h) in enumerate(pieces[1:]):
            w[e, h] = shared.tile(
                [P, HALF, PACK], BF16, name=f"w{e}{h}", offset=VALUES_AT + 2048 + 512 * i, align_bytes=64
            )
        acc = [ps.tile([P, DV // 2], F32, name=f"acc{c}", tag=f"bank{c}") for c in range(2)]

        def query_cols(h):
            return slice(h * HALF, (h + 1) * HALF)

        for e, h in pieces:
            nc.scalar.activation(
                prob[e, h][:], flipped[e][:, :, query_cols(h)].rearrange("p t q -> p q t"), ACT.Sigmoid, scale=2.0
            )

        def weigh(e, h):
            nc.vector.tensor_tensor(w[e, h][:], prob[e, h][:], vs_by_query(e), ALU.mult)

        nc.gpsimd.tensor_tensor(
            w[0, 0][:].rearrange("p q t -> p (q t)"),
            prob[0, 0][:].rearrange("p q t -> p (q t)"),
            vs_wide[:].rearrange("p q t -> p (q t)"),
            ALU.mult,
        )
        weigh(0, 1)
        weigh(1, 0)

        wq = [
            shared.tile([P, NQ], U32, name="wq0", offset=PROBS_AT + 1024, align_bytes=64),
            sb.tile([P, NQ], U32, name="wq1", align_bytes=64),
        ]
        wsc = [sb.tile([P, NQ], U8, name=f"wsc{e}", align_bytes=64) for e in range(PAGES)]

        def quantise(e, h):
            nc.vector.quantize_mx(
                out=wq[e][:, query_cols(h)].bitcast(FP8X4),
                scales=wsc[e][:, query_cols(h)],
                in_=w[e, h][:].rearrange("p q t -> p (q t)"),
            )

        def product(e):
            for c in range(2):
                vc = slice(e * DV + c * (DV // 2), e * DV + (c + 1) * (DV // 2))
                nc.tensor.matmul_mx(
                    out=acc[c][:],
                    lhsT=wq[e][:].bitcast(FP8X4),
                    lhsT_scale=wsc[e][:],
                    rhs=vg[:, vc].bitcast(FP8X4),
                    rhs_scale=v_plane[V_PLANE:P, vc],
                    start=(e == 0),
                    stop=(e == PAGES - 1),
                )

        quantise(0, 1)
        quantise(0, 0)
        product(0)
        weigh(1, 1)
        quantise(1, 0)
        quantise(1, 1)
        product(1)

        y0 = sb.tile([P, DV // 2], F32, name="y0")
        y1 = sb.tile([P, DV // 2], F32, name="y1")
        nc.vector.tensor_scalar(y0[:], acc[0][:], 1.0 / 16.0, None, ALU.mult)
        nc.sync.dma_start(out[0, :, 0 : DV // 2], y0[:])
        nc.scalar.activation(y1[:], acc[1][:], ACT.Copy, scale=1.0 / 16.0)
        nc.scalar.dma_start(out[0, :, DV // 2 : DV], y1[:])
